import numpy as np, ml_dtypes
CORES = [25,29,65,69,153,157,193,197]
N = 8
import mx_ref
BF = ml_dtypes.bfloat16
def gcols(t, e):
    v = np.concatenate([t.reshape(8, 16, -1, 4), np.zeros((8, 16, 1, 4), BF)], axis=2)
    return np.ascontiguousarray(np.stack([v[g][:, e[g]] for g in range(8)])).reshape(128, -1)
def tile(rs):
    return np.stack(rs, axis=2).reshape(128, -1).astype(BF)
def cut(t, i, w=512):
    return t[:, w * i:w * i + w]
def pick(q, e):
    c = np.concatenate([q[0].reshape(128, -1, 4), np.zeros((128, 1, 4), np.uint8)], axis=1); s = np.concatenate([q[1], np.ones((16, 1), np.uint8)], axis=1)
    return (np.ascontiguousarray(c[:, e].reshape(128, -1)), np.ascontiguousarray(s[:, e]))
def join(*qs):
    return (np.concatenate([q[0] for q in qs], axis=1), np.concatenate([q[1] for q in qs], axis=1))
def put(q, e, v):
    c, s = q[0].reshape(128, -1, 4).copy(), q[1].copy(); c[:, e] = v[0].reshape(128, -1, 4); s[:, e] = v[1]
    return (c.reshape(128, -1), s)
def pk(c, s):
    return (np.ascontiguousarray(c), mx_ref.live(s))
def emit(q):
    return q[0], q[1]
def packed(v, rng):
    q = [mx_ref.quantize(np.ascontiguousarray(v[r])) for r in range(N)]
    return np.stack([a for a, b in q]), np.stack([mx_ref.plane(b, rng) for a, b in q])
def values_of_codes():
    e, c = np.zeros((128, 128, 4), np.float32), np.zeros((128, 2, 4), np.uint8)
    e[np.arange(128), np.arange(128), 0] = 1
    c[:127, :, 0] = np.arange(256).reshape(2, 128).T[:127]
    return mx_ref.matmul(mx_ref.quantize(e.reshape(128, 512).astype(BF)), (c.reshape(128, 8), np.full((16, 2), 127, np.uint8))).T.reshape(-1).astype(np.float64)
CODE_VALUE, SCALE_VALUE = values_of_codes(), 2.0 ** (np.arange(256) - 127.0)
def decode(q):
    return (CODE_VALUE[q[0]].reshape(16, 8, -1, 4) * SCALE_VALUE[q[1]][:, None, :, None] + 0.0).reshape(128, -1).astype(np.float32)
def f(rng, *shape):
    return mx_ref.flush((rng.standard_normal(shape, dtype=np.float32) * np.exp2(rng.integers(-2, 3, shape[:-1] + (1,)))).astype(BF))
def wide(rng, *shape, cols=0):
    v = rng.standard_normal(shape, dtype=np.float32) * np.exp2(rng.integers(-12, 13, shape)).astype(np.float32)
    if cols: v *= np.repeat(np.exp2(rng.integers(-cols, cols + 1, shape[:-2] + (1, shape[-1] // 4))) * (rng.random(shape[:-2] + (1, shape[-1] // 4)) > 0.0625), 4, axis=-1).astype(np.float32)
    return mx_ref.flush(v.astype(BF))
C, K, R = 416, 64, 2
def partner(r, t):
    return r ^ (1 << t)
def highest(p):
    return np.argsort(-(p[::16] + np.float32(0.0)), axis=1, kind="stable")[:, :K]
def warp(own, other):
    n = len(own)
    rows, i = np.arange(n), np.argsort(own, axis=1)
    a, b = np.take_along_axis(own, i, axis=1), np.take_along_axis(other, i, axis=1)
    length, back = np.ones((n, K), np.int64), np.full((n, K), -1)
    for j in range(1, K):
        l = np.where(b[:, :j] < b[:, j:j + 1], length[:, :j], 0)
        best = np.argmax(l, axis=1)
        length[:, j] = 1 + l[rows, best]
        back[:, j] = np.where(l[rows, best] > 0, best, -1)
    on = np.zeros((n, K), bool)
    e = np.argmax(length, axis=1)
    for j in range(K):
        on[rows[e >= 0], e[e >= 0]] = True
        e = np.where(e >= 0, back[rows, e], -1)
    w, p = np.zeros((n, C), np.int64), np.arange(C)
    for k in range(n):
        c, d = a[k][on[k]], b[k][on[k]]
        i = np.searchsorted(c, p, side="right") - 1
        w[k] = np.where(i < 0, np.maximum(0, d[0] - c[0] + p), np.minimum(d[i] + p - c[i], np.append(d[1:] - 1, C - 1)[i]))
    return w
def clear(v):
    v = v.astype(np.float32)
    v[np.abs(v) < np.float32(2.0 ** -16)] = 0
    return v.astype(BF)
def numbers_of(rng):
    return {"x": clear(f(rng, N, 128, 4 * C)), "u": np.array(f(rng, N, 128, 512)), "v": np.array(f(rng, N, 128, 512))}
def weights(rng, w):
    c, p = packed(w, rng)
    return {"wc": c, "ws": p}
def quiet(rng, a, b):
    w = np.array(f(rng, N, 128, 2048)).reshape(N, 8, 16, 4, 8, 16, 4)
    w[:, :, 0] = 0
    w[:, :, :, :, :, :a] = 0
    w[:, :, :, :, :, b:] = 0
    return weights(rng, w.reshape(N, 128, 2048))
def signs(rng):
    return np.stack([rng.permutation(8) % 2 * 2.0 - 1.0 for r in range(N)])
def planted(d, rng, s, m, unit, k):
    x = d["x"].astype(np.float32).reshape(N, 8, 16, C, 4)
    g = ((s[..., None] >> np.arange(8)) & 1) * 2.0 ** np.arange(8) * unit[:, None, None, None]
    x[:, :, 0] = 0
    x[:, :, 0, :, 0] = m
    x[:, :, 8] = g[..., :4]
    x[:, :, 9] = g[..., 4:]
    x[:, :, 10:] = rng.integers(4, 8, (N, 8, 6, C, 4)) * rng.choice([-8.0, 8.0], (N, 8, 6, C, 4)) * unit[:, None, None, None, None]
    u = d["u"].reshape(N, 128, 128, 4)
    k = k.astype(np.float32).astype(BF)
    u[:, :, ::16] = 0
    for h in range(0, 128, 16):
        u[:, h, h, 0] = k
        u[:, h + 8:h + 10, h] = k[:, None, None]
    return {"x": x.reshape(N, 128, 4 * C).astype(BF), "u": u.reshape(N, 128, 512), "v": d["v"], **quiet(rng, 1, 8)}
def patterns(rng):
    i = np.arange(K)
    return np.stack([i, i[::-1], i + 7 - 2 * (i % 8), K - 8 - i + 2 * (i % 8), i ^ 1, rng.permutation(K), (i - 1) % K, (i + K // 2) % K])
def setup_inputs(rng):
    return {**numbers_of(rng), **weights(rng, f(rng, N, 128, 2048))}
def setup_inputs_ties(rng):
    d = numbers_of(rng)
    o = rng.permutation(N)
    x = d["x"].reshape(N, 8, 16, C, 4)
    for r in range(N):
        n = 1 if o[r] == 0 else (3, 9, 24)[o[r] % 3]
        a = x[r][:, :8, :n].copy()
        if n > 1: a[:, :, 2] = 0
        x[r][:, :8] = a[:, :, rng.permutation(C) % n]
        if o[r] == 1: x[r] = 0
    u = d["u"].reshape(N, 8, 16, 8, 16, 4)
    for h in range(8):
        a = u[:, h, :8, h, 0].copy()
        u[:, :, :, h, 0] = 0
        u[:, h, :8, h, 0] = a
    return {"x": x.reshape(N, 128, 4 * C), "u": u.reshape(N, 128, 512), "v": d["v"], **quiet(rng, 8, 16)}
def setup_inputs_near(rng):
    d = numbers_of(rng)
    s = (np.argsort(rng.random((N, 8, C)), axis=2) + 1) // 2
    tiny = (np.arange(N) // 2 + int(rng.integers(2))) % 2 == 0
    m = np.repeat((signs(rng) * ~tiny[:, None])[:, :, None], C, axis=2)
    for r in range(N):
        m[r, rng.permutation(8)[:4], rng.integers(0, C, 4)] = 2.0 ** 30 * rng.choice([-1.0, 1.0], 4)
    return planted(d, rng, s, m, np.where(tiny, 2.0 ** -29, 2.0 ** -23), np.where(tiny, 2.0 ** -30, 1.0))
def setup_inputs_chains(rng):
    d = numbers_of(rng)
    s, m = np.zeros((N, 8, C), np.int64), -1.0 * rng.integers(1, 8, (N, 8, C))
    for o in range(0, N, 4):
        k, to = rng.permutation(8), patterns(rng)
        for g in range(8):
            a, b, t = rng.permutation(K), rng.permutation(K), to[k[g]]
            four = (a, a, t[a], t[a]) if (k[g] + o // 4) % 2 == 0 else (a, t[a], b, t[b])
            for i in range(4):
                e = (np.arange(K), np.arange(C - K, C), np.sort(rng.permutation(C)[:K]))[(k[g] + i) % 3]
                m[o + i, g, e] = 0
                s[o + i, g, e[four[i]]] = K - np.arange(K)
    return planted(d, rng, s, m, np.full(N, 2.0 ** -23), np.ones(N))
def setup_inputs_huge(rng):
    d = numbers_of(rng)
    x = 2.0 ** 30 * (0.6 + 0.4 * rng.random((N, 128, C, 4)))
    c = np.stack([rng.permutation(C) % 2 * 2.0 - 1.0 for r in range(N)])
    c[rng.permutation(N) < N // 2] = 1
    x *= c[:, None, :, None]
    u = d["u"].reshape(N, 128, 128, 4)
    a = 2.0 ** 30 * (1 - 0.25 * rng.random((N, 128, 8, 4))) * signs(rng)[:, None, :, None]
    u[:, :, ::16] = a.astype(np.float32).astype(BF)
    w = np.zeros((N, 128, 4, 128, 4), np.float32)
    i = np.arange(128)
    for b in range(4): w[:, i, b, i, b] = -16
    return {"x": x.astype(np.float32).reshape(N, 128, 4 * C).astype(BF), "u": u.reshape(N, 128, 512), "v": d["v"], **weights(rng, w.reshape(N, 128, 2048).astype(BF))}
def setup_inputs_spread(rng):
    d = setup_inputs(rng)
    d["x"] = clear(wide(rng, N, 128, 4 * C, cols=6))
    return d
def check_inputs(d):
    b = []
    for k in ("x", "u", "v"):
        a = np.abs(d[k].astype(np.float32))
        if not (np.isfinite(a).all() and ((a == 0) | (a >= 2.0 ** -30) & (a <= 2.0 ** 30)).all()): b.append("a value of " + k)
    return b
def reference(x, u, v, wc, ws):
    qu = [mx_ref.quantize(u[r]) for r in range(N)]
    lay = [pk(wc[r], ws[r]) for r in range(N)]
    now = [x[r] for r in range(N)]
    y, oq = np.zeros((N, 128, C), np.float32), np.zeros((N, 8, R * C), np.float32)
    oc, osc = np.zeros((N, 128, 4 * C), np.uint8), np.zeros((N, 16, C), np.uint8)
    for t in range(R):
        state = [mx_ref.quantize(now[r]) for r in range(N)]
        top = [highest(mx_ref.matmul(qu[r], state[r])) for r in range(N)]
        held = decode(join(*state)).astype(BF)
        for r in range(N):
            e = partner(r, t)
            q = warp(top[r], top[e])
            oq[r, :, C * t:C * t + C] = q
            came = gcols(cut(held, e, 4 * C), q)
            mid = ((now[r].astype(np.float32) + came.astype(np.float32)) * np.float32(0.5)).astype(BF)
            g, z = mid.astype(np.float32), mx_ref.quantize(mid)
            now[r] = tile([g[:, b::4] + np.maximum(mx_ref.matmul(pick(lay[r], np.arange(128 * b, 128 * b + 128)), z), np.float32(0.0)) * np.float32(0.015625) for b in range(4)])
    for r in range(N):
        z = mx_ref.quantize(now[r])
        y[r] = mx_ref.matmul(mx_ref.quantize(v[r]), z)
        oc[r], osc[r] = emit(z)
    return {"y": y, "oq": oq, "oc": oc, "osc": osc}

@@ -1,0 +1,482 @@
+from concourse.mybir import dt, AluOpType, AxisListType, ActivationFunctionType
+
+C, K, R = 416, 64, 2
+H = C // 2
+W = 130
+S = K // 2
+D0 = 14
+WN = 432
+BIG = 1e29
+HALVES = ((160, 416), (0, 160))
+RUNS = ((0, 160), (160, 288), (288, 416))
+SCALAR_PIVOTS = ((4, 5, 6, 7, 8), (4, 5, 6, 7))
+X4, U8, BF, F32, I32, U16 = "float8_e4m3fn_x4", "uint8", "bfloat16", "float32", "int32", "uint16"
+
+
+def _sb(n, d):
+    return ("sbuf", [128, n], d)
+
+
+SCRATCH = {"ps": ("psum", [128, 4096], F32)}
+for _n, _w, _d in [
+    ("xa", 4 * C, BF), ("xh", 4 * C, BF), ("dh", 4 * C, BF), ("gt", 4 * C, BF), ("rl", 4 * C, F32),
+    ("ub", 512, BF), ("vb", 512, BF), ("uq", 128, X4), ("us", 128, U8), ("upq", 128, X4), ("ups", 128, U8),
+    ("vq", 128, X4), ("vs", 128, U8), ("wq", 512, X4), ("wp", 512, U8),
+    ("tq0", C, X4), ("ts0", C, U8), ("tq1", C, X4), ("ts1", C, U8), ("tq2", C, X4), ("ts2", C, U8),
+    ("lq0", C, X4), ("ls0", C, U8), ("lq1", C, X4), ("ls1", C, U8), ("rq", C, X4), ("rs", C, U8),
+    ("gq", C, X4), ("gs", C, U8), ("zs0", 128, I32), ("zs1", 128, I32), ("zl0", K, I32), ("zl1", K, I32), ("rz", K, I32),
+    ("ui", 8, I32), ("uoff", 8, U16), ("i2", C, I32), ("i2a", C, I32), ("m16", C, F32), ("m32", C, F32),
+    ("rst1", C, BF), ("rst2", 128, BF), ("ba", 512, BF), ("bt", 512, BF), ("bq", 128, X4), ("bs", 128, U8),
+    ("et", 2048, BF), ("eq", 512, X4), ("es", 512, U8), ("par", 2, I32), ("pc", 2, F32),
+    ("thr", 4, F32), ("nw", H, F32), ("rt0", K, F32), ("rt", K, F32), ("ones", 512, BF), ("zer", H, BF),
+    ("pe", H, F32), ("po", H, F32), ("wv", H, F32), ("mk", C, F32), ("hold", C, F32), ("sg", 8 * H, BF),
+    ("c1", 16 * H, BF), ("c1q", 4 * H, X4), ("c1s", 4 * H, U8), ("sel", H, BF), ("cnt", H, BF), ("junk", H, BF), ("junk2", H, BF),
+    ("acc", 4, F32), ("moff", 4, U16), ("cand", 128, F32), ("xc", 128, F32), ("mk2", 128, F32), ("hold2", 128, F32),
+    ("c2", 1536, BF), ("c2q", 384, X4), ("c2s", 384, U8), ("r2", 128, F32), ("yoff", 4, U16),
+    ("mk3", 128, F32), ("hold3", 128, F32), ("roff", 8, U16), ("zc", 128, F32), ("zr", 128, F32),
+    ("km", K, F32), ("kh", K, F32), ("koff", 4, U16), ("na", K, F32), ("am", K, F32), ("ah", K, F32),
+    ("aoff", 8, U16), ("tz", K, F32), ("th", K, F32), ("poff", 8, U16), ("nb", K, I32), ("dif", S, F32), ("bump", K, BF),
+    ("mt", S * W, BF), ("dd", D0 + (S + 1) * W, BF), ("ll", K, F32), ("ss", K, F32), ("pm", K + 1, F32),
+    ("val", 2 * K, F32), ("val2", K, F32), ("mn", 4, F32), ("wn0", 2 * WN, F32), ("wn1", 2 * WN, F32),
+    ("cap", C, F32), ("gf", C, F32), ("qq", C, F32), ("qh", C, F32), ("qoff", 26, U16), ("qo0", C, F32), ("qo1", C, F32),
+    ("yb", C, F32),
+]:
+    SCRATCH[_n] = _sb(_w, _d)
+
+SEMAPHORES = ["cV", "cS", "cP", "cG", "sent", "out", "ldxa", "ldxb", "ldu", "ldv", "ldw", "ldp", "mfill", "add0", "add1",
+              "aq0", "as0", "az0", "aq1", "as1", "az1", "fq", "fs", "fz"]
+
+A = AluOpType
+F = ActivationFunctionType
+
+
+def _relay(src, dst, cores, topo):
+    if topo.may_write(src, dst):
+        return None
+    ok = [c for c in topo.cores_of(src) if c not in cores and topo.may_write(c, dst)]
+    near = [c for c in ok if topo.die(c) == topo.die(src)]
+    return (near or ok)[0]
+
+
+def _emit(g, T, ops, tail):
+    queue = {"V": g.vector, "S": g.scalar, "P": g.tensor, "G": g, "Y": g.sync}
+    seen = {}
+    deps = []
+    for i, o in enumerate(ops):
+        d = set()
+        for name, mask, wr in o["acc"]:
+            for j, m2, w2 in seen.get(name, ()):
+                if j == i or not mask & m2:
+                    continue
+                other = ops[j]["eng"] != o["eng"]
+                if name[:3] == "ps#":
+                    if other or ((wr or w2) and not o.get("chain")):
+                        d.add(j)
+                elif wr or w2:
+                    d.add(j)
+        for name, mask, wr in o["acc"]:
+            seen.setdefault(name, []).append((i, mask, wr))
+        deps.append(d)
+    known = {e: ({}, set()) for e in queue}
+    snap, waits, marked = {}, [], set()
+    for i, o in enumerate(ops):
+        if o["eng"] is None:
+            snap[i] = ({}, set())
+            waits.append([])
+            continue
+        done, dmas = known[o["eng"]]
+        ws = []
+        for j in sorted(deps[i], reverse=True):
+            p = ops[j]
+            if p.get("sem"):
+                if p["sem"] in dmas:
+                    continue
+                dmas.add(p["sem"])
+            else:
+                if done.get(p["eng"], -1) >= j:
+                    continue
+                done[p["eng"]] = j
+                marked.add(j)
+            ws.append(j)
+            for e, v in snap[j][0].items():
+                if done.get(e, -1) < v:
+                    done[e] = v
+            dmas.update(snap[j][1])
+        waits.append(ws)
+        snap[i] = (dict(done), set(dmas))
+    count, at = {e: 0 for e in queue}, {}
+    for i, o in enumerate(ops):
+        if i in marked:
+            count[o["eng"]] += 1
+            at[i] = count[o["eng"]]
+    for i, o in enumerate(ops):
+        if o["eng"] is None:
+            continue
+        q = queue[o["eng"]]
+        for j in waits[i]:
+            p = ops[j]
+            if p.get("sem"):
+                q.wait_ge(T.sem[p["sem"]], p["n"])
+            else:
+                q.wait_ge(T.sem["c" + p["eng"]], at[j])
+        ins = o["fn"](q)
+        if o.get("inc"):
+            ins.then_inc(T.sem[o["inc"]], 16)
+        elif i in marked:
+            ins.then_inc(T.sem["c" + o["eng"]], 1)
+    for e, sem, n in tail:
+        queue[e].wait_ge(T.sem[sem], n)
+
+
+def _width(topo, src, dst):
+    return len(topo.engines(src, dst))
+
+
+def _hand_on(g, core, T, topo):
+    cores = list(T.cores)
+    for t in range(R):
+        for r, src in enumerate(cores):
+            dst = cores[r ^ (1 << t)]
+            if _relay(src, dst, cores, topo) != core:
+                continue
+            rid, pid = topo.addr(dst, core)
+            n_in, n_out, mask = _width(topo, src, core), _width(topo, core, dst), topo.mask(core, dst)
+            for sem, here, there, arr, codes in (("fq", "rq", "lq%d" % t, "aq%d" % t, True), ("fs", "rs", "ls%d" % t, "as%d" % t, False),
+                                                 ("fz", "rz", "zl%d" % t, "az%d" % t, False)):
+                g.wait_ge(T.sem[sem], n_in)
+                a, b = T[there][:], T[here][:]
+                if codes:
+                    a, b = a.bitcast(dt.uint8), b.bitcast(dt.uint8)
+                g.remote_dma(a, b, T.sem[arr], T.sem.sent, pid, rid, mask)
+            g.wait_ge(T.sem.sent, 3 * n_out)
+
+
+def rank_program(g, core, T, topo):
+    rank = T.rank_of(core)
+    if rank is None:
+        _hand_on(g, core, T, topo)
+        return
+    cores = list(T.cores)
+    ops = []
+    sent, outs = [0], [0]
+
+    def ap(name, lo=0, hi=None, step=1):
+        n = SCRATCH[name][1][1]
+        hi = n if hi is None else hi
+        mask = 0
+        if step == 1 or step == -1:
+            mask = ((1 << (hi - lo)) - 1) << lo
+        else:
+            for c in range(lo, hi, step):
+                mask |= 1 << c
+        if step == -1:
+            return (T[name][:, slice(hi - 1, lo - 1 if lo else None, -1)], [(name, mask)])
+        if step == 1:
+            return (T[name][:, lo:hi], [(name, mask)])
+        return (T[name][:, lo:hi:step], [(name, mask)])
+
+    def bank(b, lo, hi, step=1):
+        v = T.ps[:, 512 * b + lo:512 * b + hi] if step == 1 else T.ps[:, 512 * b + lo:512 * b + hi:step]
+        return (v, [("ps#%d" % b, 1)])
+
+    def ind(win, off):
+        return (win[0].indirect(off[0]), win[1] + off[1])
+
+    def add(eng, fn, writes, reads, **kw):
+        acc = [(n, m, True) for o in writes for n, m in o[1][:1]] + [(n, m, False) for o in writes for n, m in o[1][1:]]
+        acc += [(n, m, False) for o in reads if isinstance(o, tuple) for n, m in o[1]]
+        ops.append(dict(eng=eng, fn=fn, acc=acc, **kw))
+
+    def raw(o):
+        return o[0] if isinstance(o, tuple) else o
+
+    def tt(out, a, b, op):
+        add("V", lambda q: q.tensor_tensor(out[0], a[0], b[0], op), [out], [a, b])
+
+    def ts(out, a, s1, op0, s2=None, op1=None):
+        if op1 is None:
+            add("V", lambda q: q.tensor_scalar(out[0], a[0], raw(s1), None, op0), [out], [a, s1])
+        else:
+            add("V", lambda q: q.tensor_scalar(out[0], a[0], raw(s1), raw(s2), op0, op1), [out], [a, s1, s2])
+
+    def cp(out, a):
+        add("V", lambda q: q.tensor_copy(out[0], a[0]), [out], [a])
+
+    def scan(out, a, b, init, op0, op1):
+        add("V", lambda q: q.tensor_tensor_scan(out[0], a[0], b[0], raw(init), op0, op1), [out], [a, b, init])
+
+    def red(out, a, op):
+        add("V", lambda q: q.tensor_reduce(out[0], a[0], AxisListType.X, op), [out], [a])
+
+    def fill(out, v):
+        add("V", lambda q: q.memset(out[0], v), [out], [])
+
+    def quant(qn, sn, lo, hi, src):
+        a, b = ap(qn, lo, hi), ap(sn, lo, hi)
+        add("V", lambda q: q.quantize_mx(a[0], b[0], src[0]), [a, b], [src])
+
+    def act(out, a, func, bias=0.0, scale=1.0, accum=None):
+        if accum is None:
+            add("S", lambda q: q.activation(out[0], a[0], func, bias=raw(bias), scale=raw(scale)), [out], [a, bias, scale])
+        else:
+            add("S", lambda q: q.activation(out[0], a[0], func, bias=raw(bias), scale=raw(scale), accum_out=accum[0]), [out, accum], [a, bias, scale])
+
+    def mm(b, sq, ss, s0, mq, ms, lo, hi, start=True, stop=True):
+        out, a, sa, m, sm = bank(b, 0, hi - lo), ap(sq, s0, s0 + 128), ap(ss, s0, s0 + 128), ap(mq, lo, hi), ap(ms, lo, hi)
+        add("P", lambda q: q.matmul_mx(out[0], a[0], sa[0], m[0], sm[0], start, stop), [out], [a, sa, m, sm], chain=not start)
+
+    def iota(out, pattern, base, cm, small=True):
+        if small:
+            add("G", lambda q: q.iota(out[0], pattern, base, cm, allow_small_or_imprecise_dtypes=True), [out], [])
+        else:
+            add("G", lambda q: q.iota(out[0], pattern, base, cm), [out], [])
+
+    def keep(out, a, pattern, op, base, cm):
+        add("G", lambda q: q.affine_select(out[0], a[0], pattern, op, 0.0, base, cm), [out], [a])
+
+    def load(eng, out, src, sem, codes=False, after=(), n=16):
+        o = out[0].bitcast(dt.uint8) if codes else out[0]
+        add(eng, lambda q: q.dma_start(o, src), [out], list(after), sem=sem, n=n, inc=sem)
+
+    def add_into(out, a, sem):
+        add("G", lambda q: q.dma_start(out[0], a[0], accum_op=A.add), [out], [a], sem=sem, n=16, inc=sem)
+
+    def store(eng, dst, src, reads):
+        outs[0] += 16
+        add(eng, lambda q: q.dma_start(dst, src), [], [reads], inc="out", sem="out", n=0)
+
+    def send(t, here, there, hop, arr, hopsem, codes=False):
+        dst = cores[rank ^ (1 << t)]
+        via = _relay(core, dst, cores, topo)
+        to, name, sem = (dst, there, arr) if via is None else (via, hop, hopsem)
+        rid, pid = topo.addr(to, core)
+        mask = topo.mask(core, to)
+        a, b = T[name][:], here[0]
+        if codes:
+            a, b = a.bitcast(dt.uint8), b.bitcast(dt.uint8)
+        sent[0] += _width(topo, core, to)
+        add("G", lambda q: q.remote_dma(a, b, T.sem[sem], T.sem.sent, pid, rid, mask), [], [here], sem="sent", n=0)
+        back = _relay(dst, core, cores, topo)
+        add(None, None, [ap(there)], [], sem=arr, n=_width(topo, dst if back is None else back, core))
+
+    def scores(tq, tp, h):
+        lo, hi = HALVES[h]
+        mm(h, "upq", "ups", 0, tq, tp, lo, hi)
+        mm(2 + h, "upq", "ups", 0, tq, tp, lo, hi)
+
+    load("Y", ap("xa", 640, 4 * C), T.x[:, 640:4 * C], "ldxa")
+    load("S", ap("ub"), T.u[:, :], "ldu")
+    load("S", ap("xa", 0, 640), T.x[:, 0:640], "ldxb")
+    iota(ap("ui"), [[16, 8]], 0, 0, small=False)
+    iota(ap("i2"), [[-1, C]], 512, 1, small=False)
+    fill(ap("ones"), 1.0)
+    fill(ap("mt", 0, 8 * W), 0.0)
+    keep(ap("ba"), ap("ones"), [[16, 8], [0, 64]], A.is_ge, 15, -1)
+    keep(ap("bt"), ap("ba"), [[-16, 8], [0, 64]], A.is_ge, 0, 1)
+    cp(ap("uoff"), ap("ui"))
+    fill(ap("mt", 0, 8 * W, 65), -128.0)
+    ts(ap("i2a"), ap("i2"), 15, A.bitwise_and)
+    fill(ap("rst1"), 0.0)
+    ts(ap("m16"), ap("i2a"), -2 * BIG, A.mult, BIG, A.add)
+    fill(ap("rst1", 0, C, 32), -BIG)
+    act(ap("c1", 12 * H, 14 * H), ap("ones", 0, 2 * H), F.Copy, scale=0.0)
+    act(ap("c1", 14 * H, 16 * H), ap("ones", 0, 2 * H), F.Copy, scale=0.0)
+    act(ap("c2", 1024, 1536), ap("ones"), F.Copy, scale=0.0)
+    act(ap("m32", 0, C, 2), ap("m16", 0, H), F.Copy)
+    act(ap("m32", 1, C, 2), ap("m16", 0, H), F.Copy)
+    quant("uq", "us", 0, 128, ap("ub"))
+    o1, w1, o2, w2 = ap("upq"), ap("uq"), ap("ups"), ap("us")
+    add("V", lambda q: q.tensor_copy(o1[0].bitcast(dt.uint32), w1[0].bitcast(dt.uint32).indirect(T.uoff[:, 0:8])), [o1], [w1, ap("uoff")])
+    add("S", lambda q: q.activation(o2[0], w2[0].indirect(T.uoff[:, 0:8]), F.Copy), [o2], [w2, ap("uoff")])
+    for h, (lo, hi) in enumerate(HALVES):
+        quant("tq0", "ts0", lo, hi, ap("xa", 4 * lo, 4 * hi))
+        scores("tq0", "ts0", h)
+    fill(ap("zer"), 0.0)
+    fill(ap("rst2"), 0.0)
+    for k in range(1, 4):
+        load("Y", ap("mt", 8 * W * k, 8 * W * (k + 1)), T.mt[:, 0:8 * W], "mfill", after=[ap("mt", 0, 8 * W), ap("xa")], n=16 * 3)
+    load("Y", ap("wq"), T.wc[:, :], "ldw", codes=True)
+    load("Y", ap("vb"), T.v[:, :], "ldv")
+    load("G", ap("wp"), T.ws[:, :], "ldp")
+    iota(ap("nw"), [[-2, H]], 511, 0)
+    iota(ap("rt0"), [[W, S], [K, 2]], 0, 0)
+
+    def planes(row, n, hold, step, tile, qn, sn, b, aside, extra):
+        nc = n // 16
+        tiles = nc // 4 + 1
+
+        def pivot(c):
+            return ap(hold, step * 16 * (c + 1) - 1, step * 16 * (c + 1))
+
+        def part(c, lo, hi):
+            at = 4 * n * (c // 4) + c % 4
+            return ap(tile, at + 4 * lo, at + 4 * hi - 3, 4)
+
+        for k, c in enumerate(aside):
+            act(ap("sg", n * k, n * k + n), ap(row), F.Sign, bias=pivot(c), scale=-1.0)
+        for k, c in enumerate(aside):
+            e = 16 * (c + 1)
+            act(part(c, 0, e), ap("sg", n * k, n * k + e), F.Relu)
+            if e < n:
+                act(part(c, e, n), ap("sg", n * k + e, n * k + n), F.Sign, bias=1.0)
+        tt(part(nc, 0, n), ap(row), ap(hold, step - 1, step * n, step), A.is_equal)
+        extra()
+        order = sorted(range(tiles), key=lambda m: (len([c for c in aside if c // 4 == m]), -m))
+        for m in order:
+            for c in range(4 * m, min(4 * m + 4, nc)):
+                if c in aside:
+                    continue
+                e = 16 * (c + 1)
+                ts(part(c, 0, e), ap(row, 0, e), pivot(c), A.is_lt)
+                if e < n:
+                    ts(part(c, e, n), ap(row, e, n), pivot(c), A.is_le)
+            quant(qn, sn, n * m, n * m + n, ap(tile, 4 * n * m, 4 * n * m + 4 * n))
+            mm(b, "bq", "bs", 0, qn, sn, n * m, n * m + n, m == order[0], m == order[-1])
+
+    def chosen(b, n, off, first, extra):
+        ts(ap("sel", 0, n), bank(b, 0, n), K + 0.5, A.is_le)
+        first()
+        scan(ap("cnt", 0, n), ap("sel", 0, n), ap("zer", 0, n), 0.0, A.add, A.add)
+        extra()
+        for c in range(3):
+            act(ap("junk", 0, n), ap("cnt", 0, n), F.Sign, bias=ap("thr", c, c + 1), accum=ap("acc", c, c + 1))
+        ts(ap("junk2", 0, n), ap("cnt", 0, n), ap("thr", 3, 4), A.add, 0.0, A.is_lt)
+        red(ap("acc", 3, 4), ap("junk2", 0, n), A.add)
+        cp(ap(off, 3, 4), ap("acc", 3, 4))
+        ts(ap(off, 0, 3), ap("acc", 0, 3), -0.5, A.mult, n / 2, A.add)
+
+    def early():
+        quant("bq", "bs", 0, 128, ap("bt"))
+        for c in range(4):
+            ts(ap("thr", c, c + 1), ap("i2a", 0, 1), -1.0, A.mult, -0.5 - 16 * c, A.add)
+        fill(ap("rst2", 0, 128, 16), -BIG)
+
+    def nothing():
+        return None
+
+    def places():
+        tt(ap("mk3"), bank(5, 0, 128), ap("m16", 0, 128), A.min)
+
+    def listing(t):
+        act(ap("zc"), ap("cnt", 0, 128), F.Identity, bias=-1024.0, scale=1024.0)
+        scan(ap("hold3"), ap("rst2"), ap("mk3"), 0.0, A.add, A.max)
+        tt(ap("zr"), ap("zc"), ap("xc"), A.add)
+        ts(ap("roff"), ap("hold3", 15, 128, 16), -1.0, A.add)
+        cp(ind(ap("zs%d" % t), ap("roff")), ap("zr"))
+        send(t, ap("zs%d" % t, 0, K), "zl%d" % t, "rz", "az%d" % t, "fz")
+        cp(ap("r2"), bank(5, 0, 128))
+
+    state = "xa"
+    for t in range(R):
+        tq, tp, lq, lp, wn = "tq%d" % t, "ts%d" % t, "lq%d" % t, "ls%d" % t, "wn%d" % t
+        send(t, ap(tq), lq, "rq", "aq%d" % t, "fq", codes=True)
+        send(t, ap(tp), lp, "rs", "as%d" % t, "fs")
+        if t == 0:
+            for b in range(4):
+                keep(ap("et", 512 * b, 512 * b + 512), ap("ones"), [[1, 512]], A.is_equal, -b, -4)
+        for h, (lo, hi) in enumerate(HALVES):
+            act(ap("po", lo // 2, hi // 2), bank(2 + h, 1, hi - lo, 2), F.Copy)
+            tt(ap("mk", lo, hi), bank(h, 0, hi - lo), ap("m32", lo, hi), A.min)
+            if h == 0:
+                tt(ap("wv", lo // 2, hi // 2), bank(h, 0, hi - lo, 2), ap("po", lo // 2, hi // 2), A.max)
+        scan(ap("hold"), ap("rst1"), ap("mk"), 0.0, A.add, A.max)
+        tt(ap("wv", lo // 2, hi // 2), bank(h, 0, hi - lo, 2), ap("po", lo // 2, hi // 2), A.max)
+        for h, (lo, hi) in enumerate(HALVES):
+            act(ap("pe", lo // 2, hi // 2), bank(2 + h, 0, hi - lo, 2), F.Copy)
+        planes("wv", H, "hold", 2, "c1", "c1q", "c1s", 4, SCALAR_PIVOTS[0], early if t == 0 else nothing)
+        chosen(4, H, "moff", nothing, nothing)
+        cp(ap("cand", 0, 128, 2), ind(ap("pe"), ap("moff")))
+        cp(ap("cand", 1, 128, 2), ind(ap("po"), ap("moff")))
+        act(ap("xc", 0, 128, 2), ind(ap("nw"), ap("moff")), F.Copy)
+        act(ap("xc", 1, 128, 2), ind(ap("nw"), ap("moff")), F.Identity, bias=-1.0)
+        tt(ap("mk2"), ap("cand"), ap("m16", 0, 128), A.min)
+        scan(ap("hold2"), ap("rst2"), ap("mk2"), 0.0, A.add, A.max)
+        planes("cand", 128, "hold2", 1, "c2", "c2q", "c2s", 5, SCALAR_PIVOTS[1], nothing)
+        chosen(5, 128, "yoff", places, lambda: listing(t))
+        tt(ap("km"), ind(ap("r2"), ap("yoff")), ap("m16", 0, K), A.min)
+        tt(ap("am"), ind(ap("xc"), ap("yoff")), ap("m16", 0, K), A.min)
+        scan(ap("kh"), ap("rst2", 0, K), ap("km"), 0.0, A.add, A.max)
+        scan(ap("ah"), ap("rst2", 0, K), ap("am"), 0.0, A.add, A.max)
+        ts(ap("koff"), ap("kh", 15, K, 16), -1.0, A.add)
+        if t == 0:
+            act(ap("rt"), ap("rt0"), F.Copy, scale=1024.0)
+            ts(ap("par", 0, 1), ap("i2a", 0, 1), 1, A.bitwise_and)
+            fill(ap("dd", D0, D0 + W), 128.0)
+            ts(ap("pc", 0, 1), ap("par", 0, 1), -float(K), A.mult, 1.0, A.add)
+            ts(ap("pc", 1, 2), ap("par", 0, 1), float(K), A.mult, S * W - 0.5, A.add)
+        else:
+            cp(ind(ap("mt"), ap("poff")), ap("zer", 0, 128))
+        act(ap("na"), ind(ap("xc"), ap("yoff")), F.Copy)
+        ts(ap("aoff", 0, 4), ap("ah", 15, K, 16), -1.0, A.mult, 511.0, A.add)
+        ts(ap("aoff", 4, 8), ap("ah", 15, K, 16), -1.0, A.mult, 511.0 + WN, A.add)
+        if t == 0:
+            act(ap("wn0"), ap("mt", 0, 2 * WN), F.Copy, scale=0.0)
+            quant("eq", "es", 0, 512, ap("et"))
+        else:
+            quant("vq", "vs", 0, 128, ap("vb"))
+        zl = "zl%d" % t
+        tt(ap("tz"), ind(ap(zl), ap("koff")), ap("rt"), A.add)
+        scan(ap("th"), ap("m16", 0, K), ap("tz"), 0.0, A.max, A.min)
+        tt(ap("dif"), ap("tz", 1, K, 2), ap("tz", 0, K, 2), A.subtract)
+        ts(ap("poff", 0, 4), ap("th", 15, K, 16), 1.0 / 1024, A.mult, ap("pc", 0, 1), A.add)
+        ts(ap("bump", 0, K, 2), ap("dif"), 1024.0 * K, A.is_gt, 0.625, A.max)
+        ts(ap("bump", 1, K, 2), ap("dif"), 1024.0 * K, A.is_gt, 0.625, A.max)
+        ts(ap("poff", 4, 8), ap("th", 15, K, 16), -1.0 / 1024, A.mult, ap("pc", 1, 2), A.add)
+        cp(ind(ap("mt"), ap("poff", 0, 4)), ap("bump"))
+        ts(ap("nb"), ind(ap(zl), ap("koff")), 1023, A.bitwise_and)
+        cp(ind(ap("mt"), ap("poff", 4, 8)), ap("bump"))
+        for b in range(4):
+            mm(4 + b, "eq", "es", 128 * b, lq, lp, 0, C)
+        act(ap("xh"), ap(state), F.Copy, scale=0.5)
+        for b in range(4):
+            act(ap("dh", C * b, C * b + C), bank(4 + b, 0, C), F.Copy, scale=0.5)
+        if t == 0:
+            act(ap("wn1"), ap("xh", 0, 2 * WN), F.Copy, scale=0.0)
+        for j in range(S):
+            scan(ap("dd", D0 + W * (j + 1), D0 + W * (j + 2)), ap("mt", W * j, W * j + W), ap("dd", D0 + W * j, D0 + W * j + W), 0.0, A.add, A.max)
+        tab = ap("dd", D0 + W, D0 + (S + 1) * W)
+        top = ap("dd", D0 + S * W + K, D0 + S * W + K + 1)
+        act(ap("ll"), ind(tab, ap("poff", 0, 4)), F.Identity, bias=-130.0, scale=129.0 / 128)
+        cp(ap("pm", 0, 1), top)
+        tt(ap("ss"), ind(tab, ap("poff", 4, 8)), ap("ll"), A.add)
+        scan(ap("pm", 1, K + 1), ap("ss"), ap("ss"), top, A.max, A.max)
+        tt(ap("val", 0, K), ap("pm", 0, K), ap("pm", 1, K + 1), A.subtract)
+        tt(ap("val", K, 2 * K), ap("val", 0, K), ap("nb"), A.mult)
+        tt(ap("val2"), ap("val", 0, K), ap("na"), A.mult)
+        cp(ind(ap(wn), ap("aoff")), ap("val"))
+        red(ap("mn", 0, 1), ap("val", K, 2 * K), A.min)
+        act(ap("gf"), ap(wn, 0, C), F.Identity, bias=1.0 / 128, scale=-2048.0)
+        scan(ap("cap", 0, C, -1), ap(wn, 1, C + 1, -1), ap(wn, WN, WN + C, -1), (C - 1 - 511) / 128.0, A.add, A.min)
+        red(ap("mn", 1, 2), ap("val2"), A.min)
+        ts(ap("mn", 2, 3), ap("mn", 0, 1), ap("mn", 1, 2), A.subtract, -4.0, A.add)
+        scan(ap("qq"), ap("gf"), ap("cap"), ap("mn", 2, 3), A.add, A.min)
+        scan(ap("qh"), ap("m16"), ap("qq"), -100.0, A.max, A.min)
+        ts(ap("qoff"), ap("qh", 15, C, 16), 128.0, A.mult, 511.0, A.add)
+        qo = "qo%d" % t
+        act(ap(qo), ap("qq"), F.Relu, bias=511.0, scale=128.0)
+        store("Y", T.oq[:, C * t:C * t + C], T[qo][0:128:16, :], ap(qo))
+        for h, (lo, hi) in enumerate(RUNS):
+            for b in range(4):
+                tt(ap("gt", 4 * lo + b, 4 * hi, 4), ind(ap("dh", C * b, C * b + C), ap("qoff", lo // 16, hi // 16)), ap("xh", 4 * lo + b, 4 * hi, 4), A.add)
+            quant("gq", "gs", lo, hi, ap("gt", 4 * lo, 4 * hi))
+            for b in range(4):
+                mm(4 * (h % 2) + b, "wq", "wp", 128 * b, "gq", "gs", lo, hi)
+                act(ap("rl", 4 * lo + b, 4 * hi, 4), bank(4 * (h % 2) + b, 0, hi - lo), F.Relu, scale=0.015625)
+            if h == 0:
+                add_into(ap("gt", 4 * lo, 4 * hi), ap("rl", 4 * lo, 4 * hi), "add%d" % t)
+        state, tq, tp = "gt", "tq%d" % (t + 1), "ts%d" % (t + 1)
+        for h in (1, 2, 0):
+            lo, hi = RUNS[h]
+            if h:
+                tt(ap(state, 4 * lo, 4 * hi), ap("rl", 4 * lo, 4 * hi), ap("gt", 4 * lo, 4 * hi), A.add)
+            quant(tq, tp, lo, hi, ap(state, 4 * lo, 4 * hi))
+            if t == R - 1:
+                mm(h, "vq", "vs", 0, tq, tp, lo, hi)
+                store("Y", T.oc[:, 4 * lo:4 * hi], T[tq][:, lo:hi].bitcast(dt.uint8), ap(tq, lo, hi))
+                act(ap("yb", lo, hi), bank(h, 0, hi - lo), F.Copy)
+                store("S", T.y[:, lo:hi], T.yb[:, lo:hi], ap("yb", lo, hi))
+            elif h != 1:
+                scores(tq, tp, 0 if h else 1)
+    for k in range(4):
+        store("Y", T.osc[4 * k:4 * k + 4, :], T.ts2[32 * k:32 * k + 4, :], ap("ts2"))
+    _emit(g, T, ops, [("G", "sent", sent[0]), ("Y", "out", outs[0])])

@@ -7,9 +7,11 @@ S = K // 2
 D0 = 14
 WN = 432
 BIG = 1e29
-HALVES = ((160, 416), (0, 160))
-RUNS = ((0, 160), (160, 288), (288, 416))
+HALVES = ((128, 416), (0, 128))
+RUNS = ((0, 128), (128, 288), (288, 416))
 SCALAR_PIVOTS = ((4, 5, 6, 7, 8), (4, 5, 6, 7))
+SIDES = ((0, 65), (65, W))
+CYC, FIX, WAKE, DMA, HOP = 0.9, 45.0, 120.0, 2200.0, 2800.0
 X4, U8, BF, F32, I32, U16 = "float8_e4m3fn_x4", "uint8", "bfloat16", "float32", "int32", "uint16"
 
 
@@ -30,12 +32,12 @@ for _n, _w, _d in [
     ("et", 2048, BF), ("eq", 512, X4), ("es", 512, U8), ("par", 2, I32), ("pc", 2, F32),
     ("thr", 4, F32), ("nw", H, F32), ("rt0", K, F32), ("rt", K, F32), ("ones", 512, BF), ("zer", H, BF),
     ("pe", H, F32), ("po", H, F32), ("wv", H, F32), ("mk", C, F32), ("hold", C, F32), ("sg", 8 * H, BF),
-    ("c1", 16 * H, BF), ("c1q", 4 * H, X4), ("c1s", 4 * H, U8), ("sel", H, BF), ("cnt", H, BF), ("junk", H, BF), ("junk2", H, BF),
-    ("acc", 4, F32), ("moff", 4, U16), ("cand", 128, F32), ("xc", 128, F32), ("mk2", 128, F32), ("hold2", 128, F32),
+    ("c1", 16 * H, BF), ("c1q", 4 * H, X4), ("c1s", 4 * H, U8), ("sel", H, BF), ("cnt", H, BF), ("junk", 3 * H, BF), ("junk2", H, BF),
+    ("acc", 4, F32), ("moff", 4, U16), ("cand", 128, F32), ("xc", 128, F32), ("dx", 128, F32), ("mk2", 128, F32), ("hold2", 128, F32),
     ("c2", 1536, BF), ("c2q", 384, X4), ("c2s", 384, U8), ("r2", 128, F32), ("yoff", 4, U16),
-    ("mk3", 128, F32), ("hold3", 128, F32), ("roff", 8, U16), ("zc", 128, F32), ("zr", 128, F32),
+    ("mk3", 128, F32), ("hold3", 128, F32), ("roff", 8, U16), ("zr", 128, F32),
     ("km", K, F32), ("kh", K, F32), ("koff", 4, U16), ("na", K, F32), ("am", K, F32), ("ah", K, F32),
-    ("aoff", 8, U16), ("tz", K, F32), ("th", K, F32), ("poff", 8, U16), ("nb", K, I32), ("dif", S, F32), ("bump", K, BF),
+    ("aoff", 8, U16), ("tz", K, F32), ("th", K, F32), ("poff", 8, U16), ("nb", K, I32), ("dif", S, F32), ("bump", 2 * K, BF),
     ("mt", S * W, BF), ("dd", D0 + (S + 1) * W, BF), ("ll", K, F32), ("ss", K, F32), ("pm", K + 1, F32),
     ("val", 2 * K, F32), ("val2", K, F32), ("mn", 4, F32), ("wn0", 2 * WN, F32), ("wn1", 2 * WN, F32),
     ("cap", C, F32), ("gf", C, F32), ("qq", C, F32), ("qh", C, F32), ("qoff", 26, U16), ("qo0", C, F32), ("qo1", C, F32),
@@ -48,6 +50,7 @@ SEMAPHORES = ["cV", "cS", "cP", "cG", "sent", "out", "ldxa", "ldxb", "ldu", "ldv
 
 A = AluOpType
 F = ActivationFunctionType
+ORDER = {}
 
 
 def _relay(src, dst, cores, topo):
@@ -58,25 +61,84 @@ def _relay(src, dst, cores, topo):
     return (near or ok)[0]
 
 
-def _emit(g, T, ops, tail):
-    queue = {"V": g.vector, "S": g.scalar, "P": g.tensor, "G": g, "Y": g.sync}
-    seen = {}
-    deps = []
+def _needs(ops, order_too):
+    seen, deps = {}, []
     for i, o in enumerate(ops):
         d = set()
         for name, mask, wr in o["acc"]:
             for j, m2, w2 in seen.get(name, ()):
                 if j == i or not mask & m2:
                     continue
-                other = ops[j]["eng"] != o["eng"]
                 if name[:3] == "ps#":
-                    if other or ((wr or w2) and not o.get("chain")):
+                    if ops[j]["eng"] != o["eng"] or ((wr or w2) and (order_too or not o.get("chain"))):
                         d.add(j)
                 elif wr or w2:
                     d.add(j)
+        if order_too and "follow" in o:
+            d.add(o["follow"])
         for name, mask, wr in o["acc"]:
             seen.setdefault(name, []).append((i, mask, wr))
         deps.append(d)
+    return deps
+
+
+def _arrange(ops):
+    n = len(ops)
+    if n not in ORDER:
+        deps = _needs(ops, True)
+        succ = [[] for o in ops]
+        rest = [0.0] * n
+        for i in range(n - 1, -1, -1):
+            rest[i] += ops[i]["busy"] + ops[i]["late"] + WAKE
+            for j in deps[i]:
+                succ[j].append(i)
+                rest[j] = max(rest[j], rest[i])
+        best, seed = None, 12345
+        for attempt in range(60):
+            draws = []
+            for i in range(n + 2):
+                seed = (seed * 1103515245 + 12345) % 2147483648
+                draws.append(seed / 2147483648)
+            look, weight = 300 * draws[n], [rest[i] + 400 * draws[n + 1] * draws[i] for i in range(n)]
+            left, ready, free, pool, order, span = [len(d) for d in deps], [0.0] * n, {}, {}, [], 0.0
+            for i in range(n):
+                if not left[i]:
+                    pool.setdefault(ops[i]["eng"], []).append(i)
+            while len(order) < n:
+                pick = None
+                for e, l in pool.items():
+                    if not l:
+                        continue
+                    f = free.get(e, 0.0)
+                    t0 = max(f, min(ready[k] for k in l))
+                    i = max((k for k in l if ready[k] <= t0 + look), key=lambda k: weight[k])
+                    if ready[i] > t0:
+                        fit = [k for k in l if max(f, ready[k]) + ops[k]["busy"] <= ready[i] + 40]
+                        if fit:
+                            i = max(fit, key=lambda k: weight[k])
+                    if pick is None or max(f, ready[i]) < pick[0]:
+                        pick = (max(f, ready[i]), e, i)
+                s, e, i = pick
+                pool[e].remove(i)
+                order.append(i)
+                if e is not None:
+                    free[e] = s + ops[i]["busy"]
+                end = s + ops[i]["busy"] + ops[i]["late"]
+                span = max(span, end)
+                for k in succ[i]:
+                    ready[k] = max(ready[k], end + (0.0 if ops[k].get("follow") == i or (ops[k].get("chain") and e == "P") else WAKE))
+                    left[k] -= 1
+                    if not left[k]:
+                        pool.setdefault(ops[k]["eng"], []).append(k)
+            if best is None or span < best[0]:
+                best = (span, order)
+        ORDER[n] = best[1]
+    return [ops[i] for i in ORDER[n]]
+
+
+def _emit(g, T, ops, tail):
+    queue = {"V": g.vector, "S": g.scalar, "P": g.tensor, "G": g, "Y": g.sync}
+    deps = _needs(ops, False)
     known = {e: ({}, set()) for e in queue}
     snap, waits, marked = {}, [], set()
     for i, o in enumerate(ops):
@@ -161,8 +223,8 @@ def rank_program(g, core, T, topo):
     sent, outs = [0], [0]
 
     def ap(name, lo=0, hi=None, step=1):
-        n = SCRATCH[name][1][1]
-        hi = n if hi is None else hi
+        hi = SCRATCH[name][1][1] if hi is None else hi
+        kind = 2 if SCRATCH[name][2] == BF else 4
         mask = 0
         if step == 1 or step == -1:
             mask = ((1 << (hi - lo)) - 1) << lo
@@ -170,80 +232,90 @@ def rank_program(g, core, T, topo):
             for c in range(lo, hi, step):
                 mask |= 1 << c
         if step == -1:
-            return (T[name][:, slice(hi - 1, lo - 1 if lo else None, -1)], [(name, mask)])
-        if step == 1:
-            return (T[name][:, lo:hi], [(name, mask)])
-        return (T[name][:, lo:hi:step], [(name, mask)])
+            v = T[name][:, slice(hi - 1, lo - 1 if lo else None, -1)]
+        elif step == 1:
+            v = T[name][:, lo:hi]
+        else:
+            v = T[name][:, lo:hi:step]
+        return (v, [(name, mask)], len(range(lo, hi, abs(step))), kind)
 
     def bank(b, lo, hi, step=1):
         v = T.ps[:, 512 * b + lo:512 * b + hi] if step == 1 else T.ps[:, 512 * b + lo:512 * b + hi:step]
-        return (v, [("ps#%d" % b, 1)])
+        return (v, [("ps#%d" % b, 1)], len(range(lo, hi, step)), "p")
 
     def ind(win, off):
-        return (win[0].indirect(off[0]), win[1] + off[1])
+        return (win[0].indirect(off[0]), win[1] + off[1], 16 * off[2], "i")
 
-    def add(eng, fn, writes, reads, **kw):
+    def add(eng, fn, writes, reads, cycles, late=0.0, **kw):
         acc = [(n, m, True) for o in writes for n, m in o[1][:1]] + [(n, m, False) for o in writes for n, m in o[1][1:]]
         acc += [(n, m, False) for o in reads if isinstance(o, tuple) for n, m in o[1]]
-        ops.append(dict(eng=eng, fn=fn, acc=acc, **kw))
+        ops.append(dict(eng=eng, fn=fn, acc=acc, busy=cycles * CYC + FIX, late=late, **kw))
 
     def raw(o):
         return o[0] if isinstance(o, tuple) else o
 
+    def rate(out, *ins):
+        if out[3] == "i":
+            return 3.5 * out[2]
+        if ins and ins[0][3] == "i":
+            return 1.5 * out[2]
+        return (0.5 if all(o[3] == 2 for o in (out,) + ins) else 1.0) * max([out[2]] + [o[2] for o in ins])
+
     def tt(out, a, b, op):
-        add("V", lambda q: q.tensor_tensor(out[0], a[0], b[0], op), [out], [a, b])
+        add("V", lambda q: q.tensor_tensor(out[0], a[0], b[0], op), [out], [a, b], out[2] * {"i": 1.5, "p": 1.0}.get(a[3], 2.0))
 
     def ts(out, a, s1, op0, s2=None, op1=None):
         if op1 is None:
-            add("V", lambda q: q.tensor_scalar(out[0], a[0], raw(s1), None, op0), [out], [a, s1])
+            add("V", lambda q: q.tensor_scalar(out[0], a[0], raw(s1), None, op0), [out], [a, s1], rate(out, a))
         else:
-            add("V", lambda q: q.tensor_scalar(out[0], a[0], raw(s1), raw(s2), op0, op1), [out], [a, s1, s2])
+            add("V", lambda q: q.tensor_scalar(out[0], a[0], raw(s1), raw(s2), op0, op1), [out], [a, s1, s2], rate(out, a))
 
     def cp(out, a):
-        add("V", lambda q: q.tensor_copy(out[0], a[0]), [out], [a])
+        add("V", lambda q: q.tensor_copy(out[0], a[0]), [out], [a], rate(out, a))
 
     def scan(out, a, b, init, op0, op1):
-        add("V", lambda q: q.tensor_tensor_scan(out[0], a[0], b[0], raw(init), op0, op1), [out], [a, b, init])
+        add("V", lambda q: q.tensor_tensor_scan(out[0], a[0], b[0], raw(init), op0, op1), [out], [a, b, init], rate(out, a, b))
 
     def red(out, a, op):
-        add("V", lambda q: q.tensor_reduce(out[0], a[0], AxisListType.X, op), [out], [a])
+        add("V", lambda q: q.tensor_reduce(out[0], a[0], AxisListType.X, op), [out], [a], a[2])
 
     def fill(out, v):
-        add("V", lambda q: q.memset(out[0], v), [out], [])
+        add("V", lambda q: q.memset(out[0], v), [out], [], rate(out))
 
     def quant(qn, sn, lo, hi, src):
         a, b = ap(qn, lo, hi), ap(sn, lo, hi)
-        add("V", lambda q: q.quantize_mx(a[0], b[0], src[0]), [a, b], [src])
+        add("V", lambda q: q.quantize_mx(a[0], b[0], src[0]), [a, b], [src], 0.27 * src[2])
 
     def act(out, a, func, bias=0.0, scale=1.0, accum=None):
+        c = out[2] * (1.5 if a[3] == "i" else 1.0)
         if accum is None:
-            add("S", lambda q: q.activation(out[0], a[0], func, bias=raw(bias), scale=raw(scale)), [out], [a, bias, scale])
+            add("S", lambda q: q.activation(out[0], a[0], func, bias=raw(bias), scale=raw(scale)), [out], [a, bias, scale], c)
         else:
-            add("S", lambda q: q.activation(out[0], a[0], func, bias=raw(bias), scale=raw(scale), accum_out=accum[0]), [out, accum], [a, bias, scale])
+            add("S", lambda q: q.activation(out[0], a[0], func, bias=raw(bias), scale=raw(scale), accum_out=accum[0]), [out, accum], [a, bias, scale], c + 25)
 
     def mm(b, sq, ss, s0, mq, ms, lo, hi, start=True, stop=True):
         out, a, sa, m, sm = bank(b, 0, hi - lo), ap(sq, s0, s0 + 128), ap(ss, s0, s0 + 128), ap(mq, lo, hi), ap(ms, lo, hi)
-        add("P", lambda q: q.matmul_mx(out[0], a[0], sa[0], m[0], sm[0], start, stop), [out], [a, sa, m, sm], chain=not start)
+        add("P", lambda q: q.matmul_mx(out[0], a[0], sa[0], m[0], sm[0], start, stop), [out], [a, sa, m, sm], hi - lo + 16, chain=not start)
 
     def iota(out, pattern, base, cm, small=True):
         if small:
-            add("G", lambda q: q.iota(out[0], pattern, base, cm, allow_small_or_imprecise_dtypes=True), [out], [])
+            add("G", lambda q: q.iota(out[0], pattern, base, cm, allow_small_or_imprecise_dtypes=True), [out], [], 2 * out[2] + 120)
         else:
-            add("G", lambda q: q.iota(out[0], pattern, base, cm), [out], [])
+            add("G", lambda q: q.iota(out[0], pattern, base, cm), [out], [], 2 * out[2] + 120)
 
     def keep(out, a, pattern, op, base, cm):
-        add("G", lambda q: q.affine_select(out[0], a[0], pattern, op, 0.0, base, cm), [out], [a])
+        add("G", lambda q: q.affine_select(out[0], a[0], pattern, op, 0.0, base, cm), [out], [a], 2 * out[2] + 160)
 
     def load(eng, out, src, sem, codes=False, after=(), n=16):
         o = out[0].bitcast(dt.uint8) if codes else out[0]
-        add(eng, lambda q: q.dma_start(o, src), [out], list(after), sem=sem, n=n, inc=sem)
+        add(eng, lambda q: q.dma_start(o, src), [out], list(after), 60, late=DMA + out[2], sem=sem, n=n, inc=sem)
 
     def add_into(out, a, sem):
-        add("G", lambda q: q.dma_start(out[0], a[0], accum_op=A.add), [out], [a], sem=sem, n=16, inc=sem)
+        add("G", lambda q: q.dma_start(out[0], a[0], accum_op=A.add), [out], [a], 300, late=DMA + 1500, sem=sem, n=16, inc=sem)
 
     def store(eng, dst, src, reads):
         outs[0] += 16
-        add(eng, lambda q: q.dma_start(dst, src), [], [reads], inc="out", sem="out", n=0)
+        add(eng, lambda q: q.dma_start(dst, src), [], [reads], 60, late=DMA + reads[2], inc="out", sem="out", n=0)
 
     def send(t, here, there, hop, arr, hopsem, codes=False):
         dst = cores[rank ^ (1 << t)]
@@ -255,18 +327,20 @@ def rank_program(g, core, T, topo):
         if codes:
             a, b = a.bitcast(dt.uint8), b.bitcast(dt.uint8)
         sent[0] += _width(topo, core, to)
-        add("G", lambda q: q.remote_dma(a, b, T.sem[sem], T.sem.sent, pid, rid, mask), [], [here], sem="sent", n=0)
+        add("G", lambda q: q.remote_dma(a, b, T.sem[sem], T.sem.sent, pid, rid, mask), [], [here], 500, sem="sent", n=0)
         back = _relay(dst, core, cores, topo)
-        add(None, None, [ap(there)], [], sem=arr, n=_width(topo, dst if back is None else back, core))
+        add(None, None, [ap(there)], [], 0, late=(HOP + (3000.0 if codes else 0.0)) * (1 if back is None else 2), follow=len(ops) - 1,
+            sem=arr, n=_width(topo, dst if back is None else back, core))
 
     def scores(tq, tp, h):
         lo, hi = HALVES[h]
         mm(h, "upq", "ups", 0, tq, tp, lo, hi)
         mm(2 + h, "upq", "ups", 0, tq, tp, lo, hi)
 
-    load("Y", ap("xa", 640, 4 * C), T.x[:, 640:4 * C], "ldxa")
+    cut = 4 * RUNS[0][1]
+    load("Y", ap("xa", cut, 4 * C), T.x[:, cut:4 * C], "ldxa")
     load("S", ap("ub"), T.u[:, :], "ldu")
-    load("S", ap("xa", 0, 640), T.x[:, 0:640], "ldxb")
+    load("S", ap("xa", 0, cut), T.x[:, 0:cut], "ldxb")
     iota(ap("ui"), [[16, 8]], 0, 0, small=False)
     iota(ap("i2"), [[-1, C]], 512, 1, small=False)
     fill(ap("ones"), 1.0)
@@ -286,22 +360,35 @@ def rank_program(g, core, T, topo):
     act(ap("m32", 1, C, 2), ap("m16", 0, H), F.Copy)
     quant("uq", "us", 0, 128, ap("ub"))
     o1, w1, o2, w2 = ap("upq"), ap("uq"), ap("ups"), ap("us")
-    add("V", lambda q: q.tensor_copy(o1[0].bitcast(dt.uint32), w1[0].bitcast(dt.uint32).indirect(T.uoff[:, 0:8])), [o1], [w1, ap("uoff")])
-    add("S", lambda q: q.activation(o2[0], w2[0].indirect(T.uoff[:, 0:8]), F.Copy), [o2], [w2, ap("uoff")])
+    add("V", lambda q: q.tensor_copy(o1[0].bitcast(dt.uint32), w1[0].bitcast(dt.uint32).indirect(T.uoff[:, 0:8])), [o1], [w1, ap("uoff")], 200)
+    add("S", lambda q: q.activation(o2[0], w2[0].indirect(T.uoff[:, 0:8]), F.Copy), [o2], [w2, ap("uoff")], 200)
     for h, (lo, hi) in enumerate(HALVES):
         quant("tq0", "ts0", lo, hi, ap("xa", 4 * lo, 4 * hi))
         scores("tq0", "ts0", h)
     fill(ap("zer"), 0.0)
     fill(ap("rst2"), 0.0)
+    fill(ap("rst2", 0, 128, 16), -BIG)
+    fill(ap("dd", D0, D0 + W), 128.0)
     for k in range(1, 4):
         load("Y", ap("mt", 8 * W * k, 8 * W * (k + 1)), T.mt[:, 0:8 * W], "mfill", after=[ap("mt", 0, 8 * W), ap("xa")], n=16 * 3)
-    load("Y", ap("wq"), T.wc[:, :], "ldw", codes=True)
-    load("Y", ap("vb"), T.v[:, :], "ldv")
-    load("G", ap("wp"), T.ws[:, :], "ldp")
+    load("Y", ap("wq"), T.wc[:, :], "ldw", codes=True, after=[ap("xa")])
+    load("Y", ap("vb"), T.v[:, :], "ldv", after=[ap("xa")])
+    load("G", ap("wp"), T.ws[:, :], "ldp", after=[ap("xa")])
     iota(ap("nw"), [[-2, H]], 511, 0)
     iota(ap("rt0"), [[W, S], [K, 2]], 0, 0)
+    quant("bq", "bs", 0, 128, ap("bt"))
+    for c in range(4):
+        ts(ap("thr", c, c + 1), ap("i2a", 0, 1), -1.0, A.mult, -0.5 - 16 * c, A.add)
+        keep(ap("et", 512 * c, 512 * c + 512), ap("ones"), [[1, 512]], A.is_equal, -c, -4)
+    act(ap("rt"), ap("rt0"), F.Identity, bias=-512.0, scale=1024.0)
+    ts(ap("par", 0, 1), ap("i2a", 0, 1), 1, A.bitwise_and)
+    ts(ap("pc", 0, 1), ap("par", 0, 1), -float(K), A.mult, 1.0, A.add)
+    ts(ap("pc", 1, 2), ap("par", 0, 1), float(K), A.mult, S * W - 0.5, A.add)
+    for wn in ("wn0", "wn1"):
+        act(ap(wn, 0, WN), ap("ones", 0, WN), F.Copy, scale=0.0)
+        act(ap(wn, WN, 2 * WN), ap("ones", 0, WN), F.Copy, scale=0.0)
 
-    def planes(row, n, hold, step, tile, qn, sn, b, aside, extra):
+    def planes(row, n, hold, step, tile, qn, sn, b, aside):
         nc = n // 16
         tiles = nc // 4 + 1
 
@@ -313,14 +400,12 @@ def rank_program(g, core, T, topo):
             return ap(tile, at + 4 * lo, at + 4 * hi - 3, 4)
 
         for k, c in enumerate(aside):
-            act(ap("sg", n * k, n * k + n), ap(row), F.Sign, bias=pivot(c), scale=-1.0)
-        for k, c in enumerate(aside):
             e = 16 * (c + 1)
+            act(ap("sg", n * k, n * k + n), ap(row), F.Sign, bias=pivot(c), scale=-1.0)
             act(part(c, 0, e), ap("sg", n * k, n * k + e), F.Relu)
             if e < n:
                 act(part(c, e, n), ap("sg", n * k + e, n * k + n), F.Sign, bias=1.0)
         tt(part(nc, 0, n), ap(row), ap(hold, step - 1, step * n, step), A.is_equal)
-        extra()
         order = sorted(range(tiles), key=lambda m: (len([c for c in aside if c // 4 == m]), -m))
         for m in order:
             for c in range(4 * m, min(4 * m + 4, nc)):
@@ -333,107 +418,89 @@ def rank_program(g, core, T, topo):
             quant(qn, sn, n * m, n * m + n, ap(tile, 4 * n * m, 4 * n * m + 4 * n))
             mm(b, "bq", "bs", 0, qn, sn, n * m, n * m + n, m == order[0], m == order[-1])
 
-    def chosen(b, n, off, first, extra):
-        ts(ap("sel", 0, n), bank(b, 0, n), K + 0.5, A.is_le)
-        first()
-        scan(ap("cnt", 0, n), ap("sel", 0, n), ap("zer", 0, n), 0.0, A.add, A.add)
-        extra()
+    def chosen(row, n, unit, off):
         for c in range(3):
-            act(ap("junk", 0, n), ap("cnt", 0, n), F.Sign, bias=ap("thr", c, c + 1), accum=ap("acc", c, c + 1))
-        ts(ap("junk2", 0, n), ap("cnt", 0, n), ap("thr", 3, 4), A.add, 0.0, A.is_lt)
-        red(ap("acc", 3, 4), ap("junk2", 0, n), A.add)
-        cp(ap(off, 3, 4), ap("acc", 3, 4))
-        ts(ap(off, 0, 3), ap("acc", 0, 3), -0.5, A.mult, n / 2, A.add)
-
-    def early():
-        quant("bq", "bs", 0, 128, ap("bt"))
-        for c in range(4):
-            ts(ap("thr", c, c + 1), ap("i2a", 0, 1), -1.0, A.mult, -0.5 - 16 * c, A.add)
-        fill(ap("rst2", 0, 128, 16), -BIG)
-
-    def nothing():
-        return None
-
-    def places():
-        tt(ap("mk3"), bank(5, 0, 128), ap("m16", 0, 128), A.min)
-
-    def listing(t):
-        act(ap("zc"), ap("cnt", 0, 128), F.Identity, bias=-1024.0, scale=1024.0)
-        scan(ap("hold3"), ap("rst2"), ap("mk3"), 0.0, A.add, A.max)
-        tt(ap("zr"), ap("zc"), ap("xc"), A.add)
-        ts(ap("roff"), ap("hold3", 15, 128, 16), -1.0, A.add)
-        cp(ind(ap("zs%d" % t), ap("roff")), ap("zr"))
-        send(t, ap("zs%d" % t, 0, K), "zl%d" % t, "rz", "az%d" % t, "fz")
-        cp(ap("r2"), bank(5, 0, 128))
+            act(ap("junk", H * c, H * c + n), ap(row, 0, n), F.Sign, bias=ap("thr", c, c + 1), scale=unit, accum=ap("acc", c, c + 1))
+        if unit == 1.0:
+            ts(ap("junk2", 0, n), ap(row, 0, n), ap("thr", 3, 4), A.add, 0.0, A.is_lt)
+            red(ap("acc", 3, 4), ap("junk2", 0, n), A.add)
+            cp(ap(off, 3, 4), ap("acc", 3, 4))
+            ts(ap(off, 0, 3), ap("acc", 0, 3), -0.5, A.mult, n / 2, A.add)
+        else:
+            act(ap("junk2", 0, n), ap(row, 0, n), F.Sign, bias=ap("thr", 3, 4), scale=unit, accum=ap("acc", 3, 4))
+            ts(ap(off), ap("acc"), -0.5, A.mult, n / 2, A.add)
 
     state = "xa"
     for t in range(R):
         tq, tp, lq, lp, wn = "tq%d" % t, "ts%d" % t, "lq%d" % t, "ls%d" % t, "wn%d" % t
         send(t, ap(tq), lq, "rq", "aq%d" % t, "fq", codes=True)
         send(t, ap(tp), lp, "rs", "as%d" % t, "fs")
-        if t == 0:
-            for b in range(4):
-                keep(ap("et", 512 * b, 512 * b + 512), ap("ones"), [[1, 512]], A.is_equal, -b, -4)
         for h, (lo, hi) in enumerate(HALVES):
             act(ap("po", lo // 2, hi // 2), bank(2 + h, 1, hi - lo, 2), F.Copy)
             tt(ap("mk", lo, hi), bank(h, 0, hi - lo), ap("m32", lo, hi), A.min)
-            if h == 0:
-                tt(ap("wv", lo // 2, hi // 2), bank(h, 0, hi - lo, 2), ap("po", lo // 2, hi // 2), A.max)
-        scan(ap("hold"), ap("rst1"), ap("mk"), 0.0, A.add, A.max)
-        tt(ap("wv", lo // 2, hi // 2), bank(h, 0, hi - lo, 2), ap("po", lo // 2, hi // 2), A.max)
-        for h, (lo, hi) in enumerate(HALVES):
+            tt(ap("wv", lo // 2, hi // 2), bank(h, 0, hi - lo, 2), ap("po", lo // 2, hi // 2), A.max)
+            scan(ap("hold", lo, hi), ap("rst1", lo, hi), ap("mk", lo, hi), 0.0, A.add, A.max)
             act(ap("pe", lo // 2, hi // 2), bank(2 + h, 0, hi - lo, 2), F.Copy)
-        planes("wv", H, "hold", 2, "c1", "c1q", "c1s", 4, SCALAR_PIVOTS[0], early if t == 0 else nothing)
-        chosen(4, H, "moff", nothing, nothing)
-        cp(ap("cand", 0, 128, 2), ind(ap("pe"), ap("moff")))
-        cp(ap("cand", 1, 128, 2), ind(ap("po"), ap("moff")))
+        planes("wv", H, "hold", 2, "c1", "c1q", "c1s", 4, SCALAR_PIVOTS[0])
+        ts(ap("sel"), bank(4, 0, H), K + 0.5, A.is_le)
+        scan(ap("cnt"), ap("sel"), ap("zer"), 0.0, A.add, A.add)
+        chosen("cnt", H, 1.0, "moff")
+        for e, win in enumerate(("pe", "po")):
+            tt(ap("mk2", e, 128, 2), ind(ap(win), ap("moff")), ap("m16", e, 128, 2), A.min)
+            cp(ap("cand", e, 128, 2), ind(ap(win), ap("moff")))
         act(ap("xc", 0, 128, 2), ind(ap("nw"), ap("moff")), F.Copy)
         act(ap("xc", 1, 128, 2), ind(ap("nw"), ap("moff")), F.Identity, bias=-1.0)
-        tt(ap("mk2"), ap("cand"), ap("m16", 0, 128), A.min)
+        tt(ap("dx", 1, 128), ap("xc", 1, 128), ap("xc", 0, 127), A.subtract)
+        cp(ap("dx", 0, 1), ap("xc", 0, 1))
         scan(ap("hold2"), ap("rst2"), ap("mk2"), 0.0, A.add, A.max)
-        planes("cand", 128, "hold2", 1, "c2", "c2q", "c2s", 5, SCALAR_PIVOTS[1], nothing)
-        chosen(5, 128, "yoff", places, lambda: listing(t))
+        planes("cand", 128, "hold2", 1, "c2", "c2q", "c2s", 5, SCALAR_PIVOTS[1])
+        tt(ap("mk3"), bank(5, 0, 128), ap("m16", 0, 128), A.min)
+        ts(ap("sel", 0, 128), bank(5, 0, 128), K + 0.5, A.is_le, 1024.0, A.mult)
+        cp(ap("r2"), bank(5, 0, 128))
+        scan(ap("hold3"), ap("rst2"), ap("mk3"), 0.0, A.add, A.max)
+        scan(ap("zr"), ap("sel", 0, 128), ap("dx"), -512.0, A.add, A.add)
+        ts(ap("roff"), ap("hold3", 15, 128, 16), -1.0, A.add)
+        cp(ind(ap("zs%d" % t), ap("roff")), ap("zr"))
+        listed = len(ops) - 1
+        send(t, ap("zs%d" % t, 0, K), "zl%d" % t, "rz", "az%d" % t, "fz")
+        chosen("zr", 128, 1.0 / 1024, "yoff")
+        counted = len(ops) - 1
         tt(ap("km"), ind(ap("r2"), ap("yoff")), ap("m16", 0, K), A.min)
         tt(ap("am"), ind(ap("xc"), ap("yoff")), ap("m16", 0, K), A.min)
         scan(ap("kh"), ap("rst2", 0, K), ap("km"), 0.0, A.add, A.max)
         scan(ap("ah"), ap("rst2", 0, K), ap("am"), 0.0, A.add, A.max)
         ts(ap("koff"), ap("kh", 15, K, 16), -1.0, A.add)
-        if t == 0:
-            act(ap("rt"), ap("rt0"), F.Copy, scale=1024.0)
-            ts(ap("par", 0, 1), ap("i2a", 0, 1), 1, A.bitwise_and)
-            fill(ap("dd", D0, D0 + W), 128.0)
-            ts(ap("pc", 0, 1), ap("par", 0, 1), -float(K), A.mult, 1.0, A.add)
-            ts(ap("pc", 1, 2), ap("par", 0, 1), float(K), A.mult, S * W - 0.5, A.add)
-        else:
+        if t:
             cp(ind(ap("mt"), ap("poff")), ap("zer", 0, 128))
+            ops[-1]["follow"] = listed
+            quant("vq", "vs", 0, 128, ap("vb"))
+        else:
+            quant("eq", "es", 0, 512, ap("et"))
+        ops[-1]["follow"] = listed
         act(ap("na"), ind(ap("xc"), ap("yoff")), F.Copy)
         ts(ap("aoff", 0, 4), ap("ah", 15, K, 16), -1.0, A.mult, 511.0, A.add)
         ts(ap("aoff", 4, 8), ap("ah", 15, K, 16), -1.0, A.mult, 511.0 + WN, A.add)
-        if t == 0:
-            act(ap("wn0"), ap("mt", 0, 2 * WN), F.Copy, scale=0.0)
-            quant("eq", "es", 0, 512, ap("et"))
-        else:
-            quant("vq", "vs", 0, 128, ap("vb"))
         zl = "zl%d" % t
         tt(ap("tz"), ind(ap(zl), ap("koff")), ap("rt"), A.add)
         scan(ap("th"), ap("m16", 0, K), ap("tz"), 0.0, A.max, A.min)
         tt(ap("dif"), ap("tz", 1, K, 2), ap("tz", 0, K, 2), A.subtract)
         ts(ap("poff", 0, 4), ap("th", 15, K, 16), 1.0 / 1024, A.mult, ap("pc", 0, 1), A.add)
-        ts(ap("bump", 0, K, 2), ap("dif"), 1024.0 * K, A.is_gt, 0.625, A.max)
-        ts(ap("bump", 1, K, 2), ap("dif"), 1024.0 * K, A.is_gt, 0.625, A.max)
         ts(ap("poff", 4, 8), ap("th", 15, K, 16), -1.0 / 1024, A.mult, ap("pc", 1, 2), A.add)
-        cp(ind(ap("mt"), ap("poff", 0, 4)), ap("bump"))
-        ts(ap("nb"), ind(ap(zl), ap("koff")), 1023, A.bitwise_and)
-        cp(ind(ap("mt"), ap("poff", 4, 8)), ap("bump"))
+        for e in (0, 1, K, K + 1):
+            ts(ap("bump", e, e // K * K + K, 2), ap("dif"), 1024.0 * K, A.is_gt, 0.625, A.max)
+        cp(ind(ap("mt"), ap("poff")), ap("bump"))
+        ts(ap("nb"), ind(ap(zl), ap("koff")), 511, A.bitwise_and)
         for b in range(4):
             mm(4 + b, "eq", "es", 128 * b, lq, lp, 0, C)
-        act(ap("xh"), ap(state), F.Copy, scale=0.5)
-        for b in range(4):
+            ops[-1]["follow"] = listed
+            act(ap("xh", C * b, C * b + C), ap(state, C * b, C * b + C), F.Copy, scale=0.5)
+            ops[-1]["follow"] = counted
             act(ap("dh", C * b, C * b + C), bank(4 + b, 0, C), F.Copy, scale=0.5)
-        if t == 0:
-            act(ap("wn1"), ap("xh", 0, 2 * WN), F.Copy, scale=0.0)
+            ops[-1]["follow"] = counted
         for j in range(S):
-            scan(ap("dd", D0 + W * (j + 1), D0 + W * (j + 2)), ap("mt", W * j, W * j + W), ap("dd", D0 + W * j, D0 + W * j + W), 0.0, A.add, A.max)
+            for lo, hi in SIDES:
+                scan(ap("dd", D0 + W * (j + 1) + lo, D0 + W * (j + 1) + hi), ap("mt", W * j + lo, W * j + hi), ap("dd", D0 + W * j + lo, D0 + W * j + hi),
+                     0.0, A.add, A.max)
         tab = ap("dd", D0 + W, D0 + (S + 1) * W)
         top = ap("dd", D0 + S * W + K, D0 + S * W + K + 1)
         act(ap("ll"), ind(tab, ap("poff", 0, 4)), F.Identity, bias=-130.0, scale=129.0 / 128)
@@ -449,15 +516,20 @@ def rank_program(g, core, T, topo):
         scan(ap("cap", 0, C, -1), ap(wn, 1, C + 1, -1), ap(wn, WN, WN + C, -1), (C - 1 - 511) / 128.0, A.add, A.min)
         red(ap("mn", 1, 2), ap("val2"), A.min)
         ts(ap("mn", 2, 3), ap("mn", 0, 1), ap("mn", 1, 2), A.subtract, -4.0, A.add)
-        scan(ap("qq"), ap("gf"), ap("cap"), ap("mn", 2, 3), A.add, A.min)
-        scan(ap("qh"), ap("m16"), ap("qq"), -100.0, A.max, A.min)
-        ts(ap("qoff"), ap("qh", 15, C, 16), 128.0, A.mult, 511.0, A.add)
+        for lo, hi in ((0, RUNS[0][1]), (RUNS[0][1], C)):
+            scan(ap("qq", lo, hi), ap("gf", lo, hi), ap("cap", lo, hi), ap("qq", lo - 1, lo) if lo else ap("mn", 2, 3), A.add, A.min)
+            scan(ap("qh", lo, hi), ap("m16", lo, hi), ap("qq", lo, hi), -100.0, A.max, A.min)
+            ts(ap("qoff", lo // 16, hi // 16), ap("qh", lo + 15, hi, 16), 128.0, A.mult, 511.0, A.add)
         qo = "qo%d" % t
         act(ap(qo), ap("qq"), F.Relu, bias=511.0, scale=128.0)
         store("Y", T.oq[:, C * t:C * t + C], T[qo][0:128:16, :], ap(qo))
+        packed = 0
         for h, (lo, hi) in enumerate(RUNS):
             for b in range(4):
                 tt(ap("gt", 4 * lo + b, 4 * hi, 4), ind(ap("dh", C * b, C * b + C), ap("qoff", lo // 16, hi // 16)), ap("xh", 4 * lo + b, 4 * hi, 4), A.add)
+                if h and b == 1:
+                    ops[-1]["follow"] = packed
+            packed = len(ops)
             quant("gq", "gs", lo, hi, ap("gt", 4 * lo, 4 * hi))
             for b in range(4):
                 mm(4 * (h % 2) + b, "wq", "wp", 128 * b, "gq", "gs", lo, hi)
@@ -479,4 +551,4 @@ def rank_program(g, core, T, topo):
                 scores(tq, tp, 0 if h else 1)
     for k in range(4):
         store("Y", T.osc[4 * k:4 * k + 4, :], T.ts2[32 * k:32 * k + 4, :], ap("ts2"))
-    _emit(g, T, ops, [("G", "sent", sent[0]), ("Y", "out", outs[0])])
+    _emit(g, T, _arrange(ops), [("G", "sent", sent[0]), ("Y", "out", outs[0])])

@@ -4,14 +4,19 @@ C, K, R = 416, 64, 2
 H = C // 2
 W = 130
 S = K // 2
+HS = S // 2
 D0 = 14
+SEG = 2224
 WN = 432
 BIG = 1e29
-HALVES = ((128, 416), (0, 128))
+HALVES = (((128, 416), (0, 128)), ((0, 128), (128, 288), (288, 416)))
 RUNS = ((0, 128), (128, 288), (288, 416))
+BY_DMA = 128
 SCALAR_PIVOTS = ((4, 5, 6, 7, 8), (4, 5, 6, 7))
+SPLIT = True
 SIDES = ((0, 65), (65, W))
-CYC, FIX, WAKE, DMA, HOP = 0.9, 45.0, 120.0, 2200.0, 2800.0
+COST = (1.04, 15.0, 64, 120.0, 1600.0, 1700.0)
+CYC, FIX, LEAST, WAKE, DMA, HOP = COST
 X4, U8, BF, F32, I32, U16 = "float8_e4m3fn_x4", "uint8", "bfloat16", "float32", "int32", "uint16"
 
 
@@ -27,25 +32,27 @@ for _n, _w, _d in [
     ("tq0", C, X4), ("ts0", C, U8), ("tq1", C, X4), ("ts1", C, U8), ("tq2", C, X4), ("ts2", C, U8),
     ("lq0", C, X4), ("ls0", C, U8), ("lq1", C, X4), ("ls1", C, U8), ("rq", C, X4), ("rs", C, U8),
     ("gq", C, X4), ("gs", C, U8), ("zs0", 128, I32), ("zs1", 128, I32), ("zl0", K, I32), ("zl1", K, I32), ("rz", K, I32),
-    ("ui", 8, I32), ("uoff", 8, U16), ("i2", C, I32), ("i2a", C, I32), ("m16", C, F32), ("m32", C, F32),
-    ("rst1", C, BF), ("rst2", 128, BF), ("ba", 512, BF), ("bt", 512, BF), ("bq", 128, X4), ("bs", 128, U8),
-    ("et", 2048, BF), ("eq", 512, X4), ("es", 512, U8), ("par", 2, I32), ("pc", 2, F32),
+    ("ui", 8, I32), ("uoff", 8, U16), ("i2", C, I32), ("i2a", C, I32), ("m16", C, F32),
+    ("rst2", H, BF), ("ba", 512, BF), ("bt", 512, BF), ("bq", 128, X4), ("bs", 128, U8),
+    ("et", 2048, BF), ("eq", 512, X4), ("es", 512, U8), ("par", 2, I32), ("pc", 8, F32),
     ("thr", 4, F32), ("nw", H, F32), ("rt0", K, F32), ("rt", K, F32), ("ones", 512, BF), ("zer", H, BF),
-    ("pe", H, F32), ("po", H, F32), ("wv", H, F32), ("mk", C, F32), ("hold", C, F32), ("sg", 8 * H, BF),
+    ("pe", H, F32), ("po", H, F32), ("wv", H, F32), ("mk", H, F32), ("hold", H, F32), ("sg", 8 * H, BF),
     ("c1", 16 * H, BF), ("c1q", 4 * H, X4), ("c1s", 4 * H, U8), ("sel", H, BF), ("cnt", H, BF), ("junk", 3 * H, BF), ("junk2", H, BF),
     ("acc", 4, F32), ("moff", 4, U16), ("cand", 128, F32), ("xc", 128, F32), ("dx", 128, F32), ("mk2", 128, F32), ("hold2", 128, F32),
     ("c2", 1536, BF), ("c2q", 384, X4), ("c2s", 384, U8), ("r2", 128, F32), ("yoff", 4, U16),
-    ("mk3", 128, F32), ("hold3", 128, F32), ("roff", 8, U16), ("zr", 128, F32),
+    ("mk3", 128, BF), ("hold3", 128, BF), ("roff", 8, U16), ("zr", 128, F32),
     ("km", K, F32), ("kh", K, F32), ("koff", 4, U16), ("na", K, F32), ("am", K, F32), ("ah", K, F32),
     ("aoff", 8, U16), ("tz", K, F32), ("th", K, F32), ("poff", 8, U16), ("nb", K, I32), ("dif", S, F32), ("bump", 2 * K, BF),
-    ("mt", S * W, BF), ("dd", D0 + (S + 1) * W, BF), ("ll", K, F32), ("ss", K, F32), ("pm", K + 1, F32),
+    ("mt", S * W, BF), ("dd", D0 + 3 * SEG, BF), ("ll", K, F32), ("ss", K, F32), ("pm", K + 1, F32),
+    ("edge0", 2 * W, F32), ("edge", 2 * W, F32), ("neg", 2 * W, BF), ("base", 2 * W, BF), ("bias", 4, F32), ("mid", K + 1, F32),
+    ("xs", 128, F32), ("xt", 128, F32), ("xu", K, F32), ("xv", K, F32), ("xw", K, F32),
     ("val", 2 * K, F32), ("val2", K, F32), ("mn", 4, F32), ("wn0", 2 * WN, F32), ("wn1", 2 * WN, F32),
     ("cap", C, F32), ("gf", C, F32), ("qq", C, F32), ("qh", C, F32), ("qoff", 26, U16), ("qo0", C, F32), ("qo1", C, F32),
     ("yb", C, F32),
 ]:
     SCRATCH[_n] = _sb(_w, _d)
 
-SEMAPHORES = ["cV", "cS", "cP", "cG", "sent", "out", "ldxa", "ldxb", "ldu", "ldv", "ldw", "ldp", "mfill", "add0", "add1",
+SEMAPHORES = ["cV", "cS", "cP", "cG", "sent", "out", "ldxa", "ldxb", "ldu", "ldv", "ldw", "ldp", "mfill", "add00", "add01", "add10", "add11",
               "aq0", "as0", "az0", "aq1", "as1", "az1", "fq", "fs", "fz"]
 
 A = AluOpType
@@ -239,6 +246,9 @@ def rank_program(g, core, T, topo):
             v = T[name][:, lo:hi:step]
         return (v, [(name, mask)], len(range(lo, hi, abs(step))), kind)
 
+    def col(name, c):
+        return ap(name, c, c + 1)
+
     def bank(b, lo, hi, step=1):
         v = T.ps[:, 512 * b + lo:512 * b + hi] if step == 1 else T.ps[:, 512 * b + lo:512 * b + hi:step]
         return (v, [("ps#%d" % b, 1)], len(range(lo, hi, step)), "p")
@@ -249,20 +259,20 @@ def rank_program(g, core, T, topo):
     def add(eng, fn, writes, reads, cycles, late=0.0, **kw):
         acc = [(n, m, True) for o in writes for n, m in o[1][:1]] + [(n, m, False) for o in writes for n, m in o[1][1:]]
         acc += [(n, m, False) for o in reads if isinstance(o, tuple) for n, m in o[1]]
-        ops.append(dict(eng=eng, fn=fn, acc=acc, busy=cycles * CYC + FIX, late=late, **kw))
+        ops.append(dict(eng=eng, fn=fn, acc=acc, busy=max(cycles, LEAST) * CYC + FIX, late=late, **kw))
 
     def raw(o):
         return o[0] if isinstance(o, tuple) else o
 
     def rate(out, *ins):
         if out[3] == "i":
-            return 3.5 * out[2]
+            return 35 + 2.9 * out[2]
         if ins and ins[0][3] == "i":
-            return 1.5 * out[2]
+            return 35 + 1.25 * out[2]
         return (0.5 if all(o[3] == 2 for o in (out,) + ins) else 1.0) * max([out[2]] + [o[2] for o in ins])
 
     def tt(out, a, b, op):
-        add("V", lambda q: q.tensor_tensor(out[0], a[0], b[0], op), [out], [a, b], out[2] * {"i": 1.5, "p": 1.0}.get(a[3], 2.0))
+        add("V", lambda q: q.tensor_tensor(out[0], a[0], b[0], op), [out], [a, b], rate(out, a) if a[3] == "i" else out[2] * (1.0 if a[3] == "p" else 2.0))
 
     def ts(out, a, s1, op0, s2=None, op1=None):
         if op1 is None:
@@ -272,6 +282,9 @@ def rank_program(g, core, T, topo):
 
     def cp(out, a):
         add("V", lambda q: q.tensor_copy(out[0], a[0]), [out], [a], rate(out, a))
+
+    def turn(out, a):
+        add("V", lambda q: q.transpose(out[0], a[0]), [out], [a], rate(out, a))
 
     def scan(out, a, b, init, op0, op1):
         add("V", lambda q: q.tensor_tensor_scan(out[0], a[0], b[0], raw(init), op0, op1), [out], [a, b, init], rate(out, a, b))
@@ -287,7 +300,7 @@ def rank_program(g, core, T, topo):
         add("V", lambda q: q.quantize_mx(a[0], b[0], src[0]), [a, b], [src], 0.27 * src[2])
 
     def act(out, a, func, bias=0.0, scale=1.0, accum=None):
-        c = out[2] * (1.5 if a[3] == "i" else 1.0)
+        c = 50 + 1.25 * out[2] if a[3] == "i" else out[2]
         if accum is None:
             add("S", lambda q: q.activation(out[0], a[0], func, bias=raw(bias), scale=raw(scale)), [out], [a, bias, scale], c)
         else:
@@ -295,7 +308,7 @@ def rank_program(g, core, T, topo):
 
     def mm(b, sq, ss, s0, mq, ms, lo, hi, start=True, stop=True):
         out, a, sa, m, sm = bank(b, 0, hi - lo), ap(sq, s0, s0 + 128), ap(ss, s0, s0 + 128), ap(mq, lo, hi), ap(ms, lo, hi)
-        add("P", lambda q: q.matmul_mx(out[0], a[0], sa[0], m[0], sm[0], start, stop), [out], [a, sa, m, sm], hi - lo + 16, chain=not start)
+        add("P", lambda q: q.matmul_mx(out[0], a[0], sa[0], m[0], sm[0], start, stop), [out], [a, sa, m, sm], 0.6 * (hi - lo + 16), late=60.0, chain=not start)
 
     def iota(out, pattern, base, cm, small=True):
         if small:
@@ -311,7 +324,7 @@ def rank_program(g, core, T, topo):
         add(eng, lambda q: q.dma_start(o, src), [out], list(after), 60, late=DMA + out[2], sem=sem, n=n, inc=sem)
 
     def add_into(out, a, sem):
-        add("G", lambda q: q.dma_start(out[0], a[0], accum_op=A.add), [out], [a], 300, late=DMA + 1500, sem=sem, n=16, inc=sem)
+        add("G", lambda q: q.dma_start(out[0], a[0], accum_op=A.add), [out], [a], 300, late=DMA + 2.5 * out[2], sem=sem, n=16, inc=sem)
 
     def store(eng, dst, src, reads):
         outs[0] += 16
@@ -332,10 +345,13 @@ def rank_program(g, core, T, topo):
         add(None, None, [ap(there)], [], 0, late=(HOP + (3000.0 if codes else 0.0)) * (1 if back is None else 2), follow=len(ops) - 1,
             sem=arr, n=_width(topo, dst if back is None else back, core))
 
-    def scores(tq, tp, h):
-        lo, hi = HALVES[h]
+    def scores(t, tq, tp, h):
+        lo, hi = HALVES[t][h]
         mm(h, "upq", "ups", 0, tq, tp, lo, hi)
-        mm(2 + h, "upq", "ups", 0, tq, tp, lo, hi)
+        mm(5 + h, "upq", "ups", 0, tq, tp, lo, hi)
+
+    def lengths(k, row, lo=0, hi=W):
+        return ap("dd", D0 + SEG * k + W * row + lo, D0 + SEG * k + W * row + hi)
 
     cut = 4 * RUNS[0][1]
     load("Y", ap("xa", cut, 4 * C), T.x[:, cut:4 * C], "ldxa")
@@ -348,27 +364,23 @@ def rank_program(g, core, T, topo):
     keep(ap("ba"), ap("ones"), [[16, 8], [0, 64]], A.is_ge, 15, -1)
     keep(ap("bt"), ap("ba"), [[-16, 8], [0, 64]], A.is_ge, 0, 1)
     cp(ap("uoff"), ap("ui"))
-    fill(ap("mt", 0, 8 * W, 65), -128.0)
+    fill(ap("mt", 0, 8 * W, 65), -256.0)
     ts(ap("i2a"), ap("i2"), 15, A.bitwise_and)
-    fill(ap("rst1"), 0.0)
     ts(ap("m16"), ap("i2a"), -2 * BIG, A.mult, BIG, A.add)
-    fill(ap("rst1", 0, C, 32), -BIG)
     act(ap("c1", 12 * H, 14 * H), ap("ones", 0, 2 * H), F.Copy, scale=0.0)
     act(ap("c1", 14 * H, 16 * H), ap("ones", 0, 2 * H), F.Copy, scale=0.0)
     act(ap("c2", 1024, 1536), ap("ones"), F.Copy, scale=0.0)
-    act(ap("m32", 0, C, 2), ap("m16", 0, H), F.Copy)
-    act(ap("m32", 1, C, 2), ap("m16", 0, H), F.Copy)
     quant("uq", "us", 0, 128, ap("ub"))
     o1, w1, o2, w2 = ap("upq"), ap("uq"), ap("ups"), ap("us")
     add("V", lambda q: q.tensor_copy(o1[0].bitcast(dt.uint32), w1[0].bitcast(dt.uint32).indirect(T.uoff[:, 0:8])), [o1], [w1, ap("uoff")], 200)
     add("S", lambda q: q.activation(o2[0], w2[0].indirect(T.uoff[:, 0:8]), F.Copy), [o2], [w2, ap("uoff")], 200)
-    for h, (lo, hi) in enumerate(HALVES):
+    for h, (lo, hi) in enumerate(HALVES[0]):
         quant("tq0", "ts0", lo, hi, ap("xa", 4 * lo, 4 * hi))
-        scores("tq0", "ts0", h)
+        scores(0, "tq0", "ts0", h)
     fill(ap("zer"), 0.0)
     fill(ap("rst2"), 0.0)
-    fill(ap("rst2", 0, 128, 16), -BIG)
-    fill(ap("dd", D0, D0 + W), 128.0)
+    fill(ap("rst2", 0, H, 16), -BIG)
+    fill(lengths(0, 0), 128.0)
     for k in range(1, 4):
         load("Y", ap("mt", 8 * W * k, 8 * W * (k + 1)), T.mt[:, 0:8 * W], "mfill", after=[ap("mt", 0, 8 * W), ap("xa")], n=16 * 3)
     load("Y", ap("wq"), T.wc[:, :], "ldw", codes=True, after=[ap("xa")])
@@ -378,22 +390,39 @@ def rank_program(g, core, T, topo):
     iota(ap("rt0"), [[W, S], [K, 2]], 0, 0)
     quant("bq", "bs", 0, 128, ap("bt"))
     for c in range(4):
-        ts(ap("thr", c, c + 1), ap("i2a", 0, 1), -1.0, A.mult, -0.5 - 16 * c, A.add)
+        ts(col("thr", c), col("i2a", 0), -1.0, A.mult, -0.5 - 16 * c, A.add)
         keep(ap("et", 512 * c, 512 * c + 512), ap("ones"), [[1, 512]], A.is_equal, -c, -4)
     act(ap("rt"), ap("rt0"), F.Identity, bias=-512.0, scale=1024.0)
-    ts(ap("par", 0, 1), ap("i2a", 0, 1), 1, A.bitwise_and)
-    ts(ap("pc", 0, 1), ap("par", 0, 1), -float(K), A.mult, 1.0, A.add)
-    ts(ap("pc", 1, 2), ap("par", 0, 1), float(K), A.mult, S * W - 0.5, A.add)
+    ts(col("par", 0), col("i2a", 0), 1, A.bitwise_and)
+    ts(col("pc", 0), col("par", 0), -float(K), A.mult, 1.0, A.add)
+    ts(col("pc", 1), col("par", 0), float(K), A.mult, S * W - 0.5, A.add)
+    if SPLIT:
+        for k in range(2):
+            fill(lengths(k, HS + 1, 0, SEG - (HS + 1) * W), 0.0)
+            iota(ap("edge0", W * k, W * k + 65), [[1, 65]], 8 * W * (k + 2), 0)
+            iota(ap("edge0", W * k + 65, W * k + W), [[-1, 65]], 8 * W * k + K - 1, 0)
+        ts(col("pc", 2), col("i2a", 0), 65.0, A.mult, col("pc", 0), A.add)
+        ts(col("pc", 2), col("pc", 2), 1024.0, A.mult, -1024.0, A.add)
+        ts(col("pc", 3), col("par", 0), 1024.0 * (K - 1), A.mult, col("pc", 2), A.add)
+        ts(col("pc", 2), col("pc", 3), 512.0, A.add)
+        for k in range(2):
+            act(ap("edge", W * k, W * k + 65), ap("edge0", W * k, W * k + 65), F.Identity, bias=col("pc", 2), scale=1024.0)
+            act(ap("edge", W * k + 65, W * k + W), ap("edge0", W * k + 65, W * k + W), F.Identity, bias=col("pc", 3), scale=1024.0)
+        ts(col("par", 1), col("i2", 0), 16, A.bitwise_and)
+        ts(col("pc", 4), col("par", 1), 32.0, A.mult)
+        ts(col("pc", 5), col("par", 1), 32.0, A.mult, 1024.0, A.add)
+        ts(col("pc", 6), col("par", 1), -32.0, A.mult, -130.0, A.add)
+        ts(col("pc", 7), col("par", 1), -32.0, A.mult, -131.0 - 1024.0, A.add)
     for wn in ("wn0", "wn1"):
         act(ap(wn, 0, WN), ap("ones", 0, WN), F.Copy, scale=0.0)
         act(ap(wn, WN, 2 * WN), ap("ones", 0, WN), F.Copy, scale=0.0)
 
-    def planes(row, n, hold, step, tile, qn, sn, b, aside):
+    def planes(row, n, hold, tile, qn, sn, b, aside):
         nc = n // 16
         tiles = nc // 4 + 1
 
         def pivot(c):
-            return ap(hold, step * 16 * (c + 1) - 1, step * 16 * (c + 1))
+            return col(hold, 16 * c + 15)
 
         def part(c, lo, hi):
             at = 4 * n * (c // 4) + c % 4
@@ -405,7 +434,7 @@ def rank_program(g, core, T, topo):
             act(part(c, 0, e), ap("sg", n * k, n * k + e), F.Relu)
             if e < n:
                 act(part(c, e, n), ap("sg", n * k + e, n * k + n), F.Sign, bias=1.0)
-        tt(part(nc, 0, n), ap(row), ap(hold, step - 1, step * n, step), A.is_equal)
+        tt(part(nc, 0, n), ap(row), ap(hold), A.is_equal)
         order = sorted(range(tiles), key=lambda m: (len([c for c in aside if c // 4 == m]), -m))
         for m in order:
             for c in range(4 * m, min(4 * m + 4, nc)):
@@ -420,46 +449,89 @@ def rank_program(g, core, T, topo):
 
     def chosen(row, n, unit, off):
         for c in range(3):
-            act(ap("junk", H * c, H * c + n), ap(row, 0, n), F.Sign, bias=ap("thr", c, c + 1), scale=unit, accum=ap("acc", c, c + 1))
+            act(ap("junk", H * c, H * c + n), ap(row, 0, n), F.Sign, bias=col("thr", c), scale=unit, accum=col("acc", c))
         if unit == 1.0:
-            ts(ap("junk2", 0, n), ap(row, 0, n), ap("thr", 3, 4), A.add, 0.0, A.is_lt)
-            red(ap("acc", 3, 4), ap("junk2", 0, n), A.add)
-            cp(ap(off, 3, 4), ap("acc", 3, 4))
+            ts(ap("junk2", 0, n), ap(row, 0, n), col("thr", 3), A.add, 0.0, A.is_lt)
+            red(col("acc", 3), ap("junk2", 0, n), A.add)
+            cp(col(off, 3), col("acc", 3))
             ts(ap(off, 0, 3), ap("acc", 0, 3), -0.5, A.mult, n / 2, A.add)
         else:
-            act(ap("junk2", 0, n), ap(row, 0, n), F.Sign, bias=ap("thr", 3, 4), scale=unit, accum=ap("acc", 3, 4))
+            act(ap("junk2", 0, n), ap(row, 0, n), F.Sign, bias=col("thr", 3), scale=unit, accum=col("acc", 3))
             ts(ap(off), ap("acc"), -0.5, A.mult, n / 2, A.add)
+
+    def whole_chain():
+        def row(j, lo, hi):
+            return ap("dd", D0 + W * j + lo, D0 + W * j + hi)
+
+        for j in range(S):
+            for lo, hi in SIDES:
+                scan(row(j + 1, lo, hi), ap("mt", W * j + lo, W * j + hi), row(j, lo, hi), 0.0, A.add, A.max)
+        tab = ap("dd", D0 + W, D0 + (S + 1) * W)
+        act(ap("ll"), ind(tab, ap("poff", 0, 4)), F.Identity, bias=-130.0, scale=129.0 / 128)
+        cp(col("pm", 0), row(S, K, K + 1))
+        tt(ap("ss"), ind(tab, ap("poff", 4, 8)), ap("ll"), A.add)
+
+    def split_chain():
+        for k in range(2):
+            ts(lengths(k + 1, 0, 0, 65), ap("edge", W * k, W * k + 65), col("th", 16 * (k + 2) + 15), A.is_gt, 128.0, A.mult)
+            ts(lengths(k + 1, 0, 65, W), ap("edge", W * k + 65, W * k + W), col("th", 16 * k + 15), A.is_lt, 128.0, A.mult)
+            act(ap("neg", W * k, W * k + W), lengths(k + 1, 0), F.Copy, scale=-2.0)
+        for j in range(HS):
+            for k in range(3):
+                first = j + (HS if k else 0)
+                scan(lengths(k, j + 1), ap("mt", W * first, W * first + W), lengths(k, j), 0.0, A.add, A.max)
+        at = D0 + W * HS
+        for k in range(2):
+            scan(ap("base", W * k, W * k + W, -1), ap("neg", W * k, W * k + W, -1), ap("dd", at, at + W, -1), 0.0, A.add, A.max)
+        act(ap("bias", 0, 2), ap("base", 65, 2 * W, W), F.Identity, bias=col("pc", 4))
+        act(ap("bias", 2, 4), ap("base", 0, 2 * W, W), F.Identity, bias=col("pc", 5), scale=129.0 / 128)
+        tt(ap("mid"), ap("dd", at, at + 65), ap("dd", at + 65, at + W, -1), A.add)
+        red(col("pm", 0), ap("mid"), A.max)
+        ends = ap("dd", D0 + W, D0 + (HS + 1) * W)
+        act(ap("ll", 0, S), ind(ends, ap("poff", 0, 2)), F.Identity, bias=col("pc", 6), scale=129.0 / 128)
+        act(ap("ll", S, K), ind(ends, ap("poff", 6, 8)), F.Identity, bias=col("pc", 7))
+        for k in range(2):
+            at = D0 + SEG * (k + 1) + W - HS * W
+            tab = ap("dd", at, at + S * W)
+            act(ap("xs", K * k, K * k + S), ind(tab, ap("poff", 4, 6)), F.Identity, bias=col("bias", k))
+            ts(ap("xs", K * k + S, K * k + K), ind(tab, ap("poff", 2, 4)), 129.0 / 128, A.mult, col("bias", 2 + k), A.add)
+        turn(ap("xt"), ap("xs"))
+        scan(ap("xu"), ap("xt", 0, K), ap("xt", K, 2 * K), 0.0, A.max, A.max)
+        scan(ap("xv", 0, K, -1), ap("rst2", 0, K), ap("xu", 0, K, -1), 0.0, A.add, A.max)
+        turn(ap("xw"), ap("xv"))
+        tt(ap("ss"), ap("xw"), ap("ll"), A.add)
 
     state = "xa"
     for t in range(R):
         tq, tp, lq, lp, wn = "tq%d" % t, "ts%d" % t, "lq%d" % t, "ls%d" % t, "wn%d" % t
         send(t, ap(tq), lq, "rq", "aq%d" % t, "fq", codes=True)
         send(t, ap(tp), lp, "rs", "as%d" % t, "fs")
-        for h, (lo, hi) in enumerate(HALVES):
-            act(ap("po", lo // 2, hi // 2), bank(2 + h, 1, hi - lo, 2), F.Copy)
-            tt(ap("mk", lo, hi), bank(h, 0, hi - lo), ap("m32", lo, hi), A.min)
-            tt(ap("wv", lo // 2, hi // 2), bank(h, 0, hi - lo, 2), ap("po", lo // 2, hi // 2), A.max)
-            scan(ap("hold", lo, hi), ap("rst1", lo, hi), ap("mk", lo, hi), 0.0, A.add, A.max)
-            act(ap("pe", lo // 2, hi // 2), bank(2 + h, 0, hi - lo, 2), F.Copy)
-        planes("wv", H, "hold", 2, "c1", "c1q", "c1s", 4, SCALAR_PIVOTS[0])
+        for h, (lo, hi) in enumerate(HALVES[t]):
+            a, b = lo // 2, hi // 2
+            act(ap("po", a, b), bank(5 + h, 1, hi - lo, 2), F.Copy)
+            tt(ap("wv", a, b), bank(h, 0, hi - lo, 2), ap("po", a, b), A.max)
+            tt(ap("mk", a, b), ap("wv", a, b), ap("m16", a, b), A.min)
+            scan(ap("hold", a, b), ap("rst2", a, b), ap("mk", a, b), 0.0, A.add, A.max)
+            act(ap("pe", a, b), bank(5 + h, 0, hi - lo, 2), F.Copy)
+        planes("wv", H, "hold", "c1", "c1q", "c1s", 4, SCALAR_PIVOTS[0])
         ts(ap("sel"), bank(4, 0, H), K + 0.5, A.is_le)
         scan(ap("cnt"), ap("sel"), ap("zer"), 0.0, A.add, A.add)
         chosen("cnt", H, 1.0, "moff")
         for e, win in enumerate(("pe", "po")):
             tt(ap("mk2", e, 128, 2), ind(ap(win), ap("moff")), ap("m16", e, 128, 2), A.min)
-            cp(ap("cand", e, 128, 2), ind(ap(win), ap("moff")))
+            act(ap("cand", e, 128, 2), ind(ap(win), ap("moff")), F.Copy)
         act(ap("xc", 0, 128, 2), ind(ap("nw"), ap("moff")), F.Copy)
         act(ap("xc", 1, 128, 2), ind(ap("nw"), ap("moff")), F.Identity, bias=-1.0)
         tt(ap("dx", 1, 128), ap("xc", 1, 128), ap("xc", 0, 127), A.subtract)
-        cp(ap("dx", 0, 1), ap("xc", 0, 1))
-        scan(ap("hold2"), ap("rst2"), ap("mk2"), 0.0, A.add, A.max)
-        planes("cand", 128, "hold2", 1, "c2", "c2q", "c2s", 5, SCALAR_PIVOTS[1])
+        cp(col("dx", 0), col("xc", 0))
+        scan(ap("hold2"), ap("rst2", 0, 128), ap("mk2"), 0.0, A.add, A.max)
+        planes("cand", 128, "hold2", "c2", "c2q", "c2s", 5, SCALAR_PIVOTS[1])
         tt(ap("mk3"), bank(5, 0, 128), ap("m16", 0, 128), A.min)
         ts(ap("sel", 0, 128), bank(5, 0, 128), K + 0.5, A.is_le, 1024.0, A.mult)
-        cp(ap("r2"), bank(5, 0, 128))
-        scan(ap("hold3"), ap("rst2"), ap("mk3"), 0.0, A.add, A.max)
+        scan(ap("hold3"), ap("rst2", 0, 128), ap("mk3"), 0.0, A.add, A.max)
         scan(ap("zr"), ap("sel", 0, 128), ap("dx"), -512.0, A.add, A.add)
         ts(ap("roff"), ap("hold3", 15, 128, 16), -1.0, A.add)
+        act(ap("r2"), bank(5, 0, 128), F.Copy)
         cp(ind(ap("zs%d" % t), ap("roff")), ap("zr"))
         listed = len(ops) - 1
         send(t, ap("zs%d" % t, 0, K), "zl%d" % t, "rz", "az%d" % t, "fz")
@@ -484,8 +556,8 @@ def rank_program(g, core, T, topo):
         tt(ap("tz"), ind(ap(zl), ap("koff")), ap("rt"), A.add)
         scan(ap("th"), ap("m16", 0, K), ap("tz"), 0.0, A.max, A.min)
         tt(ap("dif"), ap("tz", 1, K, 2), ap("tz", 0, K, 2), A.subtract)
-        ts(ap("poff", 0, 4), ap("th", 15, K, 16), 1.0 / 1024, A.mult, ap("pc", 0, 1), A.add)
-        ts(ap("poff", 4, 8), ap("th", 15, K, 16), -1.0 / 1024, A.mult, ap("pc", 1, 2), A.add)
+        ts(ap("poff", 0, 4), ap("th", 15, K, 16), 1.0 / 1024, A.mult, col("pc", 0), A.add)
+        ts(ap("poff", 4, 8), ap("th", 15, K, 16), -1.0 / 1024, A.mult, col("pc", 1), A.add)
         for e in (0, 1, K, K + 1):
             ts(ap("bump", e, e // K * K + K, 2), ap("dif"), 1024.0 * K, A.is_gt, 0.625, A.max)
         cp(ind(ap("mt"), ap("poff")), ap("bump"))
@@ -497,27 +569,22 @@ def rank_program(g, core, T, topo):
             ops[-1]["follow"] = counted
             act(ap("dh", C * b, C * b + C), bank(4 + b, 0, C), F.Copy, scale=0.5)
             ops[-1]["follow"] = counted
-        for j in range(S):
-            for lo, hi in SIDES:
-                scan(ap("dd", D0 + W * (j + 1) + lo, D0 + W * (j + 1) + hi), ap("mt", W * j + lo, W * j + hi), ap("dd", D0 + W * j + lo, D0 + W * j + hi),
-                     0.0, A.add, A.max)
-        tab = ap("dd", D0 + W, D0 + (S + 1) * W)
-        top = ap("dd", D0 + S * W + K, D0 + S * W + K + 1)
-        act(ap("ll"), ind(tab, ap("poff", 0, 4)), F.Identity, bias=-130.0, scale=129.0 / 128)
-        cp(ap("pm", 0, 1), top)
-        tt(ap("ss"), ind(tab, ap("poff", 4, 8)), ap("ll"), A.add)
-        scan(ap("pm", 1, K + 1), ap("ss"), ap("ss"), top, A.max, A.max)
+        if SPLIT:
+            split_chain()
+        else:
+            whole_chain()
+        scan(ap("pm", 1, K + 1), ap("ss"), ap("ss"), col("pm", 0), A.max, A.max)
         tt(ap("val", 0, K), ap("pm", 0, K), ap("pm", 1, K + 1), A.subtract)
         tt(ap("val", K, 2 * K), ap("val", 0, K), ap("nb"), A.mult)
         tt(ap("val2"), ap("val", 0, K), ap("na"), A.mult)
         cp(ind(ap(wn), ap("aoff")), ap("val"))
-        red(ap("mn", 0, 1), ap("val", K, 2 * K), A.min)
+        red(col("mn", 0), ap("val", K, 2 * K), A.min)
         act(ap("gf"), ap(wn, 0, C), F.Identity, bias=1.0 / 128, scale=-2048.0)
         scan(ap("cap", 0, C, -1), ap(wn, 1, C + 1, -1), ap(wn, WN, WN + C, -1), (C - 1 - 511) / 128.0, A.add, A.min)
-        red(ap("mn", 1, 2), ap("val2"), A.min)
-        ts(ap("mn", 2, 3), ap("mn", 0, 1), ap("mn", 1, 2), A.subtract, -4.0, A.add)
+        red(col("mn", 1), ap("val2"), A.min)
+        ts(col("mn", 2), col("mn", 0), col("mn", 1), A.subtract, -4.0, A.add)
         for lo, hi in ((0, RUNS[0][1]), (RUNS[0][1], C)):
-            scan(ap("qq", lo, hi), ap("gf", lo, hi), ap("cap", lo, hi), ap("qq", lo - 1, lo) if lo else ap("mn", 2, 3), A.add, A.min)
+            scan(ap("qq", lo, hi), ap("gf", lo, hi), ap("cap", lo, hi), col("qq", lo - 1) if lo else col("mn", 2), A.add, A.min)
             scan(ap("qh", lo, hi), ap("m16", lo, hi), ap("qq", lo, hi), -100.0, A.max, A.min)
             ts(ap("qoff", lo // 16, hi // 16), ap("qh", lo + 15, hi, 16), 128.0, A.mult, 511.0, A.add)
         qo = "qo%d" % t
@@ -534,21 +601,22 @@ def rank_program(g, core, T, topo):
             for b in range(4):
                 mm(4 * (h % 2) + b, "wq", "wp", 128 * b, "gq", "gs", lo, hi)
                 act(ap("rl", 4 * lo + b, 4 * hi, 4), bank(4 * (h % 2) + b, 0, hi - lo), F.Relu, scale=0.015625)
-            if h == 0:
-                add_into(ap("gt", 4 * lo, 4 * hi), ap("rl", 4 * lo, 4 * hi), "add%d" % t)
+            if lo < BY_DMA:
+                add_into(ap("gt", 4 * lo, 4 * min(hi, BY_DMA)), ap("rl", 4 * lo, 4 * min(hi, BY_DMA)), "add%d%d" % (t, h))
+            if hi > BY_DMA:
+                for b in range(4):
+                    part = ap("gt", 4 * max(lo, BY_DMA) + b, 4 * hi, 4)
+                    tt(part, ap("rl", 4 * max(lo, BY_DMA) + b, 4 * hi, 4), part, A.add)
         state, tq, tp = "gt", "tq%d" % (t + 1), "ts%d" % (t + 1)
-        for h in (1, 2, 0):
-            lo, hi = RUNS[h]
-            if h:
-                tt(ap(state, 4 * lo, 4 * hi), ap("rl", 4 * lo, 4 * hi), ap("gt", 4 * lo, 4 * hi), A.add)
+        for h, (lo, hi) in enumerate(RUNS):
             quant(tq, tp, lo, hi, ap(state, 4 * lo, 4 * hi))
             if t == R - 1:
                 mm(h, "vq", "vs", 0, tq, tp, lo, hi)
                 store("Y", T.oc[:, 4 * lo:4 * hi], T[tq][:, lo:hi].bitcast(dt.uint8), ap(tq, lo, hi))
                 act(ap("yb", lo, hi), bank(h, 0, hi - lo), F.Copy)
                 store("S", T.y[:, lo:hi], T.yb[:, lo:hi], ap("yb", lo, hi))
-            elif h != 1:
-                scores(tq, tp, 0 if h else 1)
+            else:
+                scores(t + 1, tq, tp, h)
     for k in range(4):
         store("Y", T.osc[4 * k:4 * k + 4, :], T.ts2[32 * k:32 * k + 4, :], ap("ts2"))
     _emit(g, T, _arrange(ops), [("G", "sent", sent[0]), ("Y", "out", outs[0])])

@@ -9,13 +9,16 @@ D0 = 14
 SEG = 2224
 WN = 432
 BIG = 1e29
+UP = 513.0 / 512
 HALVES = (((128, 416), (0, 128)), ((0, 128), (128, 288), (288, 416)))
 RUNS = ((0, 128), (128, 288), (288, 416))
 BY_DMA = 128
-SCALAR_PIVOTS = ((4, 5, 6, 7, 8), (4, 5, 6, 7))
+SCALAR_PIVOTS = ((3, 4, 5, 6, 7, 8), (5, 6, 7))
+COUNTS = 3
+DIRECT = ((1,), (2,))
 SPLIT = True
 SIDES = ((0, 65), (65, W))
-COST = (1.04, 15.0, 64, 120.0, 1600.0, 1700.0)
+COST = (1.04, 0.0, 64, 160.0, 1500.0, 1600.0)
 CYC, FIX, LEAST, WAKE, DMA, HOP = COST
 X4, U8, BF, F32, I32, U16 = "float8_e4m3fn_x4", "uint8", "bfloat16", "float32", "int32", "uint16"
 
@@ -33,22 +36,21 @@ for _n, _w, _d in [
     ("lq0", C, X4), ("ls0", C, U8), ("lq1", C, X4), ("ls1", C, U8), ("rq", C, X4), ("rs", C, U8),
     ("gq", C, X4), ("gs", C, U8), ("zs0", 128, I32), ("zs1", 128, I32), ("zl0", K, I32), ("zl1", K, I32), ("rz", K, I32),
     ("ui", 8, I32), ("uoff", 8, U16), ("i2", C, I32), ("i2a", C, I32), ("m16", C, F32),
-    ("rst2", H, BF), ("ba", 512, BF), ("bt", 512, BF), ("bq", 128, X4), ("bs", 128, U8),
+    ("m32", 288, F32), ("rst1", 288, BF), ("rst2", H, BF), ("ba", 512, BF), ("bt", 512, BF), ("bq", 128, X4), ("bs", 128, U8),
     ("et", 2048, BF), ("eq", 512, X4), ("es", 512, U8), ("par", 2, I32), ("pc", 8, F32),
-    ("thr", 4, F32), ("nw", H, F32), ("rt0", K, F32), ("rt", K, F32), ("ones", 512, BF), ("zer", H, BF),
-    ("pe", H, F32), ("po", H, F32), ("wv", H, F32), ("mk", H, F32), ("hold", H, F32), ("sg", 8 * H, BF),
-    ("c1", 16 * H, BF), ("c1q", 4 * H, X4), ("c1s", 4 * H, U8), ("sel", H, BF), ("cnt", H, BF), ("junk", 3 * H, BF), ("junk2", H, BF),
+    ("thr", 4, F32), ("nw", H, F32), ("rt", 2 * K, F32), ("ones", 512, BF), ("zer", H, BF),
+    ("pe", H, F32), ("po", H, F32), ("wv", H, F32), ("mk", C, F32), ("hold", C, F32), ("sg", 8 * H, BF),
+    ("c1", 16 * H, BF), ("c1q", 4 * H, X4), ("c1s", 4 * H, U8), ("sel", H, BF), ("cnt", H, BF), ("junk", 4 * H, BF), ("junk2", 2 * H, BF),
     ("acc", 4, F32), ("moff", 4, U16), ("cand", 128, F32), ("xc", 128, F32), ("dx", 128, F32), ("mk2", 128, F32), ("hold2", 128, F32),
     ("c2", 1536, BF), ("c2q", 384, X4), ("c2s", 384, U8), ("r2", 128, F32), ("yoff", 4, U16),
     ("mk3", 128, BF), ("hold3", 128, BF), ("roff", 8, U16), ("zr", 128, F32),
     ("km", K, F32), ("kh", K, F32), ("koff", 4, U16), ("na", K, F32), ("am", K, F32), ("ah", K, F32),
     ("aoff", 8, U16), ("tz", K, F32), ("th", K, F32), ("poff", 8, U16), ("nb", K, I32), ("dif", S, F32), ("bump", 2 * K, BF),
     ("mt", S * W, BF), ("dd", D0 + 3 * SEG, BF), ("ll", K, F32), ("ss", K, F32), ("pm", K + 1, F32),
-    ("edge0", 2 * W, F32), ("edge", 2 * W, F32), ("neg", 2 * W, BF), ("base", 2 * W, BF), ("bias", 4, F32), ("mid", K + 1, F32),
-    ("xs", 128, F32), ("xt", 128, F32), ("xu", K, F32), ("xv", K, F32), ("xw", K, F32),
-    ("val", 2 * K, F32), ("val2", K, F32), ("mn", 4, F32), ("wn0", 2 * WN, F32), ("wn1", 2 * WN, F32),
-    ("cap", C, F32), ("gf", C, F32), ("qq", C, F32), ("qh", C, F32), ("qoff", 26, U16), ("qo0", C, F32), ("qo1", C, F32),
-    ("yb", C, F32),
+    ("keep", K, F32), ("bc", K, F32), ("edge", 4 * W, F32), ("neg", 2 * W, BF), ("base", 2 * W, BF), ("mid", K + 2, F32),
+    ("xs", 128, F32), ("xt", 128, F32), ("xu", 128, F32), ("xv", 128, F32), ("xw", K, F32), ("lt", 128, F32), ("rst3", 128, BF),
+    ("val", 2 * K, F32), ("wn0", 2 * WN, BF), ("wn1", 2 * WN, BF), ("m16b", C, BF),
+    ("cap", C, BF), ("gf", C, BF), ("qq", C, BF), ("qh", C, BF), ("qoff", 26, U16), ("qo", R * C, F32), ("yb", C, F32),
 ]:
     SCRATCH[_n] = _sb(_w, _d)
 
@@ -380,6 +382,10 @@ def rank_program(g, core, T, topo):
     fill(ap("zer"), 0.0)
     fill(ap("rst2"), 0.0)
     fill(ap("rst2", 0, H, 16), -BIG)
+    wide = max(HALVES[t][h][1] - HALVES[t][h][0] for t in range(R) for h in DIRECT[t])
+    for e in range(2):
+        act(ap("m32", e, wide, 2), ap("m16", 0, wide // 2), F.Copy)
+        act(ap("rst1", e, wide, 2), ap("rst2", 0, wide // 2), F.Copy, scale=1.0 - e)
     fill(lengths(0, 0), 128.0)
     for k in range(1, 4):
         load("Y", ap("mt", 8 * W * k, 8 * W * (k + 1)), T.mt[:, 0:8 * W], "mfill", after=[ap("mt", 0, 8 * W), ap("xa")], n=16 * 3)
@@ -387,42 +393,45 @@ def rank_program(g, core, T, topo):
     load("Y", ap("vb"), T.v[:, :], "ldv", after=[ap("xa")])
     load("G", ap("wp"), T.ws[:, :], "ldp", after=[ap("xa")])
     iota(ap("nw"), [[-2, H]], 511, 0)
-    iota(ap("rt0"), [[W, S], [K, 2]], 0, 0)
+    iota(ap("rt", K, 2 * K), [[W, S], [K, 2]], 0, 0)
     quant("bq", "bs", 0, 128, ap("bt"))
     for c in range(4):
         ts(col("thr", c), col("i2a", 0), -1.0, A.mult, -0.5 - 16 * c, A.add)
         keep(ap("et", 512 * c, 512 * c + 512), ap("ones"), [[1, 512]], A.is_equal, -c, -4)
-    act(ap("rt"), ap("rt0"), F.Identity, bias=-512.0, scale=1024.0)
+    act(ap("rt", 0, K), ap("rt", K, 2 * K), F.Identity, bias=-512.0, scale=1024.0)
     ts(col("par", 0), col("i2a", 0), 1, A.bitwise_and)
     ts(col("pc", 0), col("par", 0), -float(K), A.mult, 1.0, A.add)
     ts(col("pc", 1), col("par", 0), float(K), A.mult, S * W - 0.5, A.add)
     if SPLIT:
         for k in range(2):
             fill(lengths(k, HS + 1, 0, SEG - (HS + 1) * W), 0.0)
-            iota(ap("edge0", W * k, W * k + 65), [[1, 65]], 8 * W * (k + 2), 0)
-            iota(ap("edge0", W * k + 65, W * k + W), [[-1, 65]], 8 * W * k + K - 1, 0)
+            iota(ap("edge", W * (k + 2), W * (k + 2) + 65), [[1, 65]], 8 * W * (k + 2), 0)
+            iota(ap("edge", W * (k + 2) + 65, W * (k + 3)), [[-1, 65]], 8 * W * k + K - 1, 0)
         ts(col("pc", 2), col("i2a", 0), 65.0, A.mult, col("pc", 0), A.add)
         ts(col("pc", 2), col("pc", 2), 1024.0, A.mult, -1024.0, A.add)
         ts(col("pc", 3), col("par", 0), 1024.0 * (K - 1), A.mult, col("pc", 2), A.add)
         ts(col("pc", 2), col("pc", 3), 512.0, A.add)
         for k in range(2):
-            act(ap("edge", W * k, W * k + 65), ap("edge0", W * k, W * k + 65), F.Identity, bias=col("pc", 2), scale=1024.0)
-            act(ap("edge", W * k + 65, W * k + W), ap("edge0", W * k + 65, W * k + W), F.Identity, bias=col("pc", 3), scale=1024.0)
-        ts(col("par", 1), col("i2", 0), 16, A.bitwise_and)
-        ts(col("pc", 4), col("par", 1), 32.0, A.mult)
-        ts(col("pc", 5), col("par", 1), 32.0, A.mult, 1024.0, A.add)
-        ts(col("pc", 6), col("par", 1), -32.0, A.mult, -130.0, A.add)
-        ts(col("pc", 7), col("par", 1), -32.0, A.mult, -131.0 - 1024.0, A.add)
+            act(ap("edge", W * k, W * k + 65), ap("edge", W * (k + 2), W * (k + 2) + 65), F.Identity, bias=col("pc", 2), scale=1024.0)
+            act(ap("edge", W * k + 65, W * k + W), ap("edge", W * (k + 2) + 65, W * (k + 3)), F.Identity, bias=col("pc", 3), scale=1024.0)
+        ts(col("pc", 4), col("i2a", 0), 15.0, A.is_equal)
+        for c, v in ((5, UP), (6, -128.25), (7, -128.5)):
+            act(col("pc", c), col("pc", 4), F.Copy, scale=v)
+        fill(ap("rst3"), 0.0)
+        fill(ap("rst3", 0, 128, 32), -BIG)
+        fill(ap("lt", 1, 128, 2), 0.0)
+        fill(ap("lt", 31, 128, 32), -BIG)
+    act(ap("m16b"), ap("m16"), F.Copy)
     for wn in ("wn0", "wn1"):
         act(ap(wn, 0, WN), ap("ones", 0, WN), F.Copy, scale=0.0)
-        act(ap(wn, WN, 2 * WN), ap("ones", 0, WN), F.Copy, scale=0.0)
+        act(ap(wn, WN, 2 * WN), ap("ones", 0, WN), F.Copy)
 
-    def planes(row, n, hold, tile, qn, sn, b, aside):
+    def planes(row, n, hold, step, tile, qn, sn, b, aside):
         nc = n // 16
         tiles = nc // 4 + 1
 
         def pivot(c):
-            return col(hold, 16 * c + 15)
+            return col(hold, step * 16 * (c + 1) - 1)
 
         def part(c, lo, hi):
             at = 4 * n * (c // 4) + c % 4
@@ -434,7 +443,7 @@ def rank_program(g, core, T, topo):
             act(part(c, 0, e), ap("sg", n * k, n * k + e), F.Relu)
             if e < n:
                 act(part(c, e, n), ap("sg", n * k + e, n * k + n), F.Sign, bias=1.0)
-        tt(part(nc, 0, n), ap(row), ap(hold), A.is_equal)
+        tt(part(nc, 0, n), ap(row), ap(hold, step - 1, step * n, step), A.is_equal)
         order = sorted(range(tiles), key=lambda m: (len([c for c in aside if c // 4 == m]), -m))
         for m in order:
             for c in range(4 * m, min(4 * m + 4, nc)):
@@ -447,29 +456,17 @@ def rank_program(g, core, T, topo):
             quant(qn, sn, n * m, n * m + n, ap(tile, 4 * n * m, 4 * n * m + 4 * n))
             mm(b, "bq", "bs", 0, qn, sn, n * m, n * m + n, m == order[0], m == order[-1])
 
-    def chosen(row, n, unit, off):
-        for c in range(3):
-            act(ap("junk", H * c, H * c + n), ap(row, 0, n), F.Sign, bias=col("thr", c), scale=unit, accum=col("acc", c))
-        if unit == 1.0:
-            ts(ap("junk2", 0, n), ap(row, 0, n), col("thr", 3), A.add, 0.0, A.is_lt)
-            red(col("acc", 3), ap("junk2", 0, n), A.add)
-            cp(col(off, 3), col("acc", 3))
-            ts(ap(off, 0, 3), ap("acc", 0, 3), -0.5, A.mult, n / 2, A.add)
-        else:
-            act(ap("junk2", 0, n), ap(row, 0, n), F.Sign, bias=col("thr", 3), scale=unit, accum=col("acc", 3))
-            ts(ap(off), ap("acc"), -0.5, A.mult, n / 2, A.add)
-
-    def whole_chain():
-        def row(j, lo, hi):
-            return ap("dd", D0 + W * j + lo, D0 + W * j + hi)
-
-        for j in range(S):
-            for lo, hi in SIDES:
-                scan(row(j + 1, lo, hi), ap("mt", W * j + lo, W * j + hi), row(j, lo, hi), 0.0, A.add, A.max)
-        tab = ap("dd", D0 + W, D0 + (S + 1) * W)
-        act(ap("ll"), ind(tab, ap("poff", 0, 4)), F.Identity, bias=-130.0, scale=129.0 / 128)
-        cp(col("pm", 0), row(S, K, K + 1))
-        tt(ap("ss"), ind(tab, ap("poff", 4, 8)), ap("ll"), A.add)
+    def chosen(row, n, unit, off, on_scalar):
+        w = n - K + 16
+        for c in range(4):
+            junk = ap("junk", H * c, H * c + w)
+            if c < on_scalar:
+                act(junk, ap(row, 16 * c, 16 * c + w), F.Sign, bias=col("thr", c), scale=unit, accum=col("acc", c))
+                ts(col(off, c), col("acc", c), -0.5, A.mult, 16 * c + w / 2, A.add)
+            else:
+                ts(junk, ap(row, 16 * c, 16 * c + w), col("thr", c), A.add, 0.0, A.is_lt)
+                scan(ap("junk2", H * (c % 2), H * (c % 2) + w), junk, ap("zer", 0, w), 16.0 * c, A.add, A.add)
+                cp(col(off, c), col("junk2", H * (c % 2) + w - 1))
 
     def split_chain():
         for k in range(2):
@@ -483,23 +480,22 @@ def rank_program(g, core, T, topo):
         at = D0 + W * HS
         for k in range(2):
             scan(ap("base", W * k, W * k + W, -1), ap("neg", W * k, W * k + W, -1), ap("dd", at, at + W, -1), 0.0, A.add, A.max)
-        act(ap("bias", 0, 2), ap("base", 65, 2 * W, W), F.Identity, bias=col("pc", 4))
-        act(ap("bias", 2, 4), ap("base", 0, 2 * W, W), F.Identity, bias=col("pc", 5), scale=129.0 / 128)
-        tt(ap("mid"), ap("dd", at, at + 65), ap("dd", at + 65, at + W, -1), A.add)
-        red(col("pm", 0), ap("mid"), A.max)
+        tt(ap("mid", 0, 65), ap("dd", at, at + 65), ap("dd", at + 65, at + W, -1), A.add)
+        red(col("mid", 65), ap("mid", 0, 65), A.max)
+        act(col("pm", 0), col("mid", 65), F.Identity, bias=1.0)
         ends = ap("dd", D0 + W, D0 + (HS + 1) * W)
-        act(ap("ll", 0, S), ind(ends, ap("poff", 0, 2)), F.Identity, bias=col("pc", 6), scale=129.0 / 128)
-        act(ap("ll", S, K), ind(ends, ap("poff", 6, 8)), F.Identity, bias=col("pc", 7))
+        act(ap("ll", 0, S), ind(ends, ap("poff", 0, 2)), F.Identity, bias=col("pc", 6), scale=col("pc", 5))
+        act(ap("ll", S, K), ind(ends, ap("poff", 6, 8)), F.Identity, bias=col("pc", 7), scale=col("pc", 4))
+        turn(ap("lt", 0, 128, 2), ap("ll"))
         for k in range(2):
             at = D0 + SEG * (k + 1) + W - HS * W
             tab = ap("dd", at, at + S * W)
-            act(ap("xs", K * k, K * k + S), ind(tab, ap("poff", 4, 6)), F.Identity, bias=col("bias", k))
-            ts(ap("xs", K * k + S, K * k + K), ind(tab, ap("poff", 2, 4)), 129.0 / 128, A.mult, col("bias", 2 + k), A.add)
-        turn(ap("xt"), ap("xs"))
-        scan(ap("xu"), ap("xt", 0, K), ap("xt", K, 2 * K), 0.0, A.max, A.max)
-        scan(ap("xv", 0, K, -1), ap("rst2", 0, K), ap("xu", 0, K, -1), 0.0, A.add, A.max)
-        turn(ap("xw"), ap("xv"))
-        tt(ap("ss"), ap("xw"), ap("ll"), A.add)
+            act(ap("xs", K * k, K * k + S), ind(tab, ap("poff", 4, 6)), F.Identity, bias=col("base", W * k + 65))
+            ts(ap("xs", K * k + S, K * k + K), ind(tab, ap("poff", 2, 4)), col("base", W * k), A.add, UP, A.mult)
+            turn(ap("xt", k, 128, 2), ap("xs", K * k, K * k + K))
+        scan(ap("xu"), ap("rst3"), ap("xt"), 0.0, A.add, A.max)
+        scan(ap("xv", 0, 128, -1), ap("lt", 0, 128, -1), ap("xu", 0, 128, -1), 0.0, A.add, A.max)
+        turn(ap("ss"), ap("xv", 0, 128, 2))
 
     state = "xa"
     for t in range(R):
@@ -510,13 +506,17 @@ def rank_program(g, core, T, topo):
             a, b = lo // 2, hi // 2
             act(ap("po", a, b), bank(5 + h, 1, hi - lo, 2), F.Copy)
             tt(ap("wv", a, b), bank(h, 0, hi - lo, 2), ap("po", a, b), A.max)
-            tt(ap("mk", a, b), ap("wv", a, b), ap("m16", a, b), A.min)
-            scan(ap("hold", a, b), ap("rst2", a, b), ap("mk", a, b), 0.0, A.add, A.max)
+            if h in DIRECT[t]:
+                tt(ap("mk", lo, hi), bank(h, 0, hi - lo), ap("m32", 0, hi - lo), A.min)
+                scan(ap("hold", lo, hi), ap("rst1", 0, hi - lo), ap("mk", lo, hi), 0.0, A.add, A.max)
+            else:
+                tt(ap("mk", lo, lo + b - a), ap("wv", a, b), ap("m16", a, b), A.min)
+                scan(ap("hold", lo + 1, hi, 2), ap("rst2", a, b), ap("mk", lo, lo + b - a), 0.0, A.add, A.max)
             act(ap("pe", a, b), bank(5 + h, 0, hi - lo, 2), F.Copy)
-        planes("wv", H, "hold", "c1", "c1q", "c1s", 4, SCALAR_PIVOTS[0])
+        planes("wv", H, "hold", 2, "c1", "c1q", "c1s", 4, SCALAR_PIVOTS[0])
         ts(ap("sel"), bank(4, 0, H), K + 0.5, A.is_le)
         scan(ap("cnt"), ap("sel"), ap("zer"), 0.0, A.add, A.add)
-        chosen("cnt", H, 1.0, "moff")
+        chosen("cnt", H, 1.0, "moff", COUNTS)
         for e, win in enumerate(("pe", "po")):
             tt(ap("mk2", e, 128, 2), ind(ap(win), ap("moff")), ap("m16", e, 128, 2), A.min)
             act(ap("cand", e, 128, 2), ind(ap(win), ap("moff")), F.Copy)
@@ -525,7 +525,7 @@ def rank_program(g, core, T, topo):
         tt(ap("dx", 1, 128), ap("xc", 1, 128), ap("xc", 0, 127), A.subtract)
         cp(col("dx", 0), col("xc", 0))
         scan(ap("hold2"), ap("rst2", 0, 128), ap("mk2"), 0.0, A.add, A.max)
-        planes("cand", 128, "hold2", "c2", "c2q", "c2s", 5, SCALAR_PIVOTS[1])
+        planes("cand", 128, "hold2", 1, "c2", "c2q", "c2s", 5, SCALAR_PIVOTS[1])
         tt(ap("mk3"), bank(5, 0, 128), ap("m16", 0, 128), A.min)
         ts(ap("sel", 0, 128), bank(5, 0, 128), K + 0.5, A.is_le, 1024.0, A.mult)
         scan(ap("hold3"), ap("rst2", 0, 128), ap("mk3"), 0.0, A.add, A.max)
@@ -535,7 +535,7 @@ def rank_program(g, core, T, topo):
         cp(ind(ap("zs%d" % t), ap("roff")), ap("zr"))
         listed = len(ops) - 1
         send(t, ap("zs%d" % t, 0, K), "zl%d" % t, "rz", "az%d" % t, "fz")
-        chosen("zr", 128, 1.0 / 1024, "yoff")
+        chosen("zr", 128, 1.0 / 1024, "yoff", 4)
         counted = len(ops) - 1
         tt(ap("km"), ind(ap("r2"), ap("yoff")), ap("m16", 0, K), A.min)
         tt(ap("am"), ind(ap("xc"), ap("yoff")), ap("m16", 0, K), A.min)
@@ -549,11 +549,11 @@ def rank_program(g, core, T, topo):
         else:
             quant("eq", "es", 0, 512, ap("et"))
         ops[-1]["follow"] = listed
-        act(ap("na"), ind(ap("xc"), ap("yoff")), F.Copy)
+        act(ap("na"), ind(ap("xc"), ap("yoff")), F.Identity, bias=H + 1.0, scale=-1.0)
         ts(ap("aoff", 0, 4), ap("ah", 15, K, 16), -1.0, A.mult, 511.0, A.add)
         ts(ap("aoff", 4, 8), ap("ah", 15, K, 16), -1.0, A.mult, 511.0 + WN, A.add)
         zl = "zl%d" % t
-        tt(ap("tz"), ind(ap(zl), ap("koff")), ap("rt"), A.add)
+        tt(ap("tz"), ind(ap(zl), ap("koff")), ap("rt", 0, K), A.add)
         scan(ap("th"), ap("m16", 0, K), ap("tz"), 0.0, A.max, A.min)
         tt(ap("dif"), ap("tz", 1, K, 2), ap("tz", 0, K, 2), A.subtract)
         ts(ap("poff", 0, 4), ap("th", 15, K, 16), 1.0 / 1024, A.mult, col("pc", 0), A.add)
@@ -562,6 +562,8 @@ def rank_program(g, core, T, topo):
             ts(ap("bump", e, e // K * K + K, 2), ap("dif"), 1024.0 * K, A.is_gt, 0.625, A.max)
         cp(ind(ap("mt"), ap("poff")), ap("bump"))
         ts(ap("nb"), ind(ap(zl), ap("koff")), 511, A.bitwise_and)
+        tt(ap("km"), ap("nb"), ap("na"), A.add)
+        ts(ap("bc"), ap("nb"), -1.0 / 512, A.mult, (511.0 - H) / 512, A.add)
         for b in range(4):
             mm(4 + b, "eq", "es", 128 * b, lq, lp, 0, C)
             ops[-1]["follow"] = listed
@@ -569,27 +571,22 @@ def rank_program(g, core, T, topo):
             ops[-1]["follow"] = counted
             act(ap("dh", C * b, C * b + C), bank(4 + b, 0, C), F.Copy, scale=0.5)
             ops[-1]["follow"] = counted
-        if SPLIT:
-            split_chain()
-        else:
-            whole_chain()
+        split_chain()
         scan(ap("pm", 1, K + 1), ap("ss"), ap("ss"), col("pm", 0), A.max, A.max)
+        tt(ap("keep"), ap("pm", 0, K), ap("pm", 1, K + 1), A.is_equal)
         tt(ap("val", 0, K), ap("pm", 0, K), ap("pm", 1, K + 1), A.subtract)
-        tt(ap("val", K, 2 * K), ap("val", 0, K), ap("nb"), A.mult)
-        tt(ap("val2"), ap("val", 0, K), ap("na"), A.mult)
+        tt(ap("val", K, 2 * K), ap("keep"), ap("bc"), A.add)
+        tt(ap("ll"), ap("val", 0, K), ap("km"), A.mult)
         cp(ind(ap(wn), ap("aoff")), ap("val"))
-        red(col("mn", 0), ap("val", K, 2 * K), A.min)
-        act(ap("gf"), ap(wn, 0, C), F.Identity, bias=1.0 / 128, scale=-2048.0)
-        scan(ap("cap", 0, C, -1), ap(wn, 1, C + 1, -1), ap(wn, WN, WN + C, -1), (C - 1 - 511) / 128.0, A.add, A.min)
-        red(col("mn", 1), ap("val2"), A.min)
-        ts(col("mn", 2), col("mn", 0), col("mn", 1), A.subtract, -4.0, A.add)
-        for lo, hi in ((0, RUNS[0][1]), (RUNS[0][1], C)):
-            scan(ap("qq", lo, hi), ap("gf", lo, hi), ap("cap", lo, hi), col("qq", lo - 1) if lo else col("mn", 2), A.add, A.min)
-            scan(ap("qh", lo, hi), ap("m16", lo, hi), ap("qq", lo, hi), -100.0, A.max, A.min)
-            ts(ap("qoff", lo // 16, hi // 16), ap("qh", lo + 15, hi, 16), 128.0, A.mult, 511.0, A.add)
-        qo = "qo%d" % t
-        act(ap(qo), ap("qq"), F.Relu, bias=511.0, scale=128.0)
-        store("Y", T.oq[:, C * t:C * t + C], T[qo][0:128:16, :], ap(qo))
+        scan(ap("xw", 0, K, -1), ap("keep", 0, K, -1), ap("ll", 0, K, -1), 0.0, A.mult, A.add)
+        scan(ap("cap", 0, C, -1), ap(wn, 1, C + 1, -1), ap(wn, WN, WN + C, -1), (C - 1 - H) / 512.0, A.add, A.min)
+        for lo, hi, qq, first in ((0, 128, "xu", col("xw", 0)), (128, C, "qq", col("xu", 127))):
+            act(ap("gf", lo, hi), ap(wn, lo, hi), F.Identity, bias=1.0 / 512, scale=-8192.0)
+            scan(ap(qq, lo, hi), ap("gf", lo, hi), ap("cap", lo, hi), first, A.add, A.min)
+            scan(ap("qh", lo, hi), ap("m16b", lo, hi), ap(qq, lo, hi), -100.0, A.max, A.min)
+            ts(ap("qoff", lo // 16, hi // 16), ap("qh", lo + 15, hi, 16), 512.0, A.mult, float(H), A.add)
+            act(ap("qo", C * t + lo, C * t + hi), ap(qq, lo, hi), F.Relu, bias=float(H), scale=512.0)
+        store("Y", T.oq[:, C * t:C * t + C], T.qo[0:128:16, C * t:C * t + C], ap("qo", C * t, C * t + C))
         packed = 0
         for h, (lo, hi) in enumerate(RUNS):
             for b in range(4):

from concourse.mybir import dt, AluOpType, AxisListType, ActivationFunctionType

C, K, R = 416, 64, 2
H = C // 2
W = 130
S = K // 2
HS = S // 2
D0 = 14
SEG = 2224
WN = 432
BIG = 1e29
UP = 513.0 / 512
HALVES = (((128, 416), (0, 128)), ((0, 128), (128, 288), (288, 416)))
RUNS = ((0, 128), (128, 288), (288, 416))
BY_DMA = 128
SCALAR_PIVOTS = ((3, 4, 5, 6, 7, 8), (5, 6, 7))
COUNTS = 3
DIRECT = ((1,), (2,))
SPLIT = True
SIDES = ((0, 65), (65, W))
COST = (1.04, 0.0, 64, 160.0, 1500.0, 1600.0)
CYC, FIX, LEAST, WAKE, DMA, HOP = COST
X4, U8, BF, F32, I32, U16 = "float8_e4m3fn_x4", "uint8", "bfloat16", "float32", "int32", "uint16"


def _sb(n, d):
    return ("sbuf", [128, n], d)


SCRATCH = {"ps": ("psum", [128, 4096], F32)}
for _n, _w, _d in [
    ("xa", 4 * C, BF), ("xh", 4 * C, BF), ("dh", 4 * C, BF), ("gt", 4 * C, BF), ("rl", 4 * C, F32),
    ("ub", 512, BF), ("vb", 512, BF), ("uq", 128, X4), ("us", 128, U8), ("upq", 128, X4), ("ups", 128, U8),
    ("vq", 128, X4), ("vs", 128, U8), ("wq", 512, X4), ("wp", 512, U8),
    ("tq0", C, X4), ("ts0", C, U8), ("tq1", C, X4), ("ts1", C, U8), ("tq2", C, X4), ("ts2", C, U8),
    ("lq0", C, X4), ("ls0", C, U8), ("lq1", C, X4), ("ls1", C, U8), ("rq", C, X4), ("rs", C, U8),
    ("gq", C, X4), ("gs", C, U8), ("zs0", 128, I32), ("zs1", 128, I32), ("zl0", K, I32), ("zl1", K, I32), ("rz", K, I32),
    ("ui", 8, I32), ("uoff", 8, U16), ("i2", C, I32), ("i2a", C, I32), ("m16", C, F32),
    ("m32", 288, F32), ("rst1", 288, BF), ("rst2", H, BF), ("ba", 512, BF), ("bt", 512, BF), ("bq", 128, X4), ("bs", 128, U8),
    ("et", 2048, BF), ("eq", 512, X4), ("es", 512, U8), ("par", 2, I32), ("pc", 8, F32),
    ("thr", 4, F32), ("nw", H, F32), ("rt", 2 * K, F32), ("ones", 512, BF), ("zer", H, BF),
    ("pe", H, F32), ("po", H, F32), ("wv", H, F32), ("mk", C, F32), ("hold", C, F32), ("sg", 8 * H, BF),
    ("c1", 16 * H, BF), ("c1q", 4 * H, X4), ("c1s", 4 * H, U8), ("sel", H, BF), ("cnt", H, BF), ("junk", 4 * H, BF), ("junk2", 2 * H, BF),
    ("acc", 4, F32), ("moff", 4, U16), ("cand", 128, F32), ("xc", 128, F32), ("dx", 128, F32), ("mk2", 128, F32), ("hold2", 128, F32),
    ("c2", 1536, BF), ("c2q", 384, X4), ("c2s", 384, U8), ("r2", 128, F32), ("yoff", 4, U16),
    ("mk3", 128, BF), ("hold3", 128, BF), ("roff", 8, U16), ("zr", 128, F32),
    ("km", K, F32), ("kh", K, F32), ("koff", 4, U16), ("na", K, F32), ("am", K, F32), ("ah", K, F32),
    ("aoff", 8, U16), ("tz", K, F32), ("th", K, F32), ("poff", 8, U16), ("nb", K, I32), ("dif", S, F32), ("bump", 2 * K, BF),
    ("mt", S * W, BF), ("dd", D0 + 3 * SEG, BF), ("ll", K, F32), ("ss", K, F32), ("pm", K + 1, F32),
    ("keep", K, F32), ("bc", K, F32), ("edge", 4 * W, F32), ("neg", 2 * W, BF), ("base", 2 * W, BF), ("mid", K + 2, F32),
    ("xs", 128, F32), ("xt", 128, F32), ("xu", 128, F32), ("xv", 128, F32), ("xw", K, F32), ("lt", 128, F32), ("rst3", 128, BF),
    ("val", 2 * K, F32), ("wn0", 2 * WN, BF), ("wn1", 2 * WN, BF), ("m16b", C, BF),
    ("cap", C, BF), ("gf", C, BF), ("qq", C, BF), ("qh", C, BF), ("qoff", 26, U16), ("qo", R * C, F32), ("yb", C, F32),
]:
    SCRATCH[_n] = _sb(_w, _d)

SEMAPHORES = ["cV", "cS", "cP", "cG", "sent", "out", "ldxa", "ldxb", "ldu", "ldv", "ldw", "ldp", "mfill", "add00", "add01", "add10", "add11",
              "aq0", "as0", "az0", "aq1", "as1", "az1", "fq", "fs", "fz"]

A = AluOpType
F = ActivationFunctionType
ORDER = {}


def _relay(src, dst, cores, topo):
    if topo.may_write(src, dst):
        return None
    ok = [c for c in topo.cores_of(src) if c not in cores and topo.may_write(c, dst)]
    near = [c for c in ok if topo.die(c) == topo.die(src)]
    return (near or ok)[0]


def _needs(ops, order_too):
    seen, deps = {}, []
    for i, o in enumerate(ops):
        d = set()
        for name, mask, wr in o["acc"]:
            for j, m2, w2 in seen.get(name, ()):
                if j == i or not mask & m2:
                    continue
                if name[:3] == "ps#":
                    if ops[j]["eng"] != o["eng"] or ((wr or w2) and (order_too or not o.get("chain"))):
                        d.add(j)
                elif wr or w2:
                    d.add(j)
        if order_too and "follow" in o:
            d.add(o["follow"])
        for name, mask, wr in o["acc"]:
            seen.setdefault(name, []).append((i, mask, wr))
        deps.append(d)
    return deps


def _arrange(ops):
    n = len(ops)
    if n not in ORDER:
        deps = _needs(ops, True)
        succ = [[] for o in ops]
        rest = [0.0] * n
        for i in range(n - 1, -1, -1):
            rest[i] += ops[i]["busy"] + ops[i]["late"] + WAKE
            for j in deps[i]:
                succ[j].append(i)
                rest[j] = max(rest[j], rest[i])
        best, seed = None, 12345
        for attempt in range(60):
            draws = []
            for i in range(n + 2):
                seed = (seed * 1103515245 + 12345) % 2147483648
                draws.append(seed / 2147483648)
            look, weight = 300 * draws[n], [rest[i] + 400 * draws[n + 1] * draws[i] for i in range(n)]
            left, ready, free, pool, order, span = [len(d) for d in deps], [0.0] * n, {}, {}, [], 0.0
            for i in range(n):
                if not left[i]:
                    pool.setdefault(ops[i]["eng"], []).append(i)
            while len(order) < n:
                pick = None
                for e, l in pool.items():
                    if not l:
                        continue
                    f = free.get(e, 0.0)
                    t0 = max(f, min(ready[k] for k in l))
                    i = max((k for k in l if ready[k] <= t0 + look), key=lambda k: weight[k])
                    if ready[i] > t0:
                        fit = [k for k in l if max(f, ready[k]) + ops[k]["busy"] <= ready[i] + 40]
                        if fit:
                            i = max(fit, key=lambda k: weight[k])
                    if pick is None or max(f, ready[i]) < pick[0]:
                        pick = (max(f, ready[i]), e, i)
                s, e, i = pick
                pool[e].remove(i)
                order.append(i)
                if e is not None:
                    free[e] = s + ops[i]["busy"]
                end = s + ops[i]["busy"] + ops[i]["late"]
                span = max(span, end)
                for k in succ[i]:
                    ready[k] = max(ready[k], end + (0.0 if ops[k].get("follow") == i or (ops[k].get("chain") and e == "P") else WAKE))
                    left[k] -= 1
                    if not left[k]:
                        pool.setdefault(ops[k]["eng"], []).append(k)
            if best is None or span < best[0]:
                best = (span, order)
        ORDER[n] = best[1]
    return [ops[i] for i in ORDER[n]]


def _emit(g, T, ops, tail):
    queue = {"V": g.vector, "S": g.scalar, "P": g.tensor, "G": g, "Y": g.sync}
    deps = _needs(ops, False)
    known = {e: ({}, set()) for e in queue}
    snap, waits, marked = {}, [], set()
    for i, o in enumerate(ops):
        if o["eng"] is None:
            snap[i] = ({}, set())
            waits.append([])
            continue
        done, dmas = known[o["eng"]]
        ws = []
        for j in sorted(deps[i], reverse=True):
            p = ops[j]
            if p.get("sem"):
                if p["sem"] in dmas:
                    continue
                dmas.add(p["sem"])
            else:
                if done.get(p["eng"], -1) >= j:
                    continue
                done[p["eng"]] = j
                marked.add(j)
            ws.append(j)
            for e, v in snap[j][0].items():
                if done.get(e, -1) < v:
                    done[e] = v
            dmas.update(snap[j][1])
        waits.append(ws)
        snap[i] = (dict(done), set(dmas))
    count, at = {e: 0 for e in queue}, {}
    for i, o in enumerate(ops):
        if i in marked:
            count[o["eng"]] += 1
            at[i] = count[o["eng"]]
    for i, o in enumerate(ops):
        if o["eng"] is None:
            continue
        q = queue[o["eng"]]
        for j in waits[i]:
            p = ops[j]
            if p.get("sem"):
                q.wait_ge(T.sem[p["sem"]], p["n"])
            else:
                q.wait_ge(T.sem["c" + p["eng"]], at[j])
        ins = o["fn"](q)
        if o.get("inc"):
            ins.then_inc(T.sem[o["inc"]], 16)
        elif i in marked:
            ins.then_inc(T.sem["c" + o["eng"]], 1)
    for e, sem, n in tail:
        queue[e].wait_ge(T.sem[sem], n)


def _width(topo, src, dst):
    return len(topo.engines(src, dst))


def _hand_on(g, core, T, topo):
    cores = list(T.cores)
    for t in range(R):
        for r, src in enumerate(cores):
            dst = cores[r ^ (1 << t)]
            if _relay(src, dst, cores, topo) != core:
                continue
            rid, pid = topo.addr(dst, core)
            n_in, n_out, mask = _width(topo, src, core), _width(topo, core, dst), topo.mask(core, dst)
            for sem, here, there, arr, codes in (("fq", "rq", "lq%d" % t, "aq%d" % t, True), ("fs", "rs", "ls%d" % t, "as%d" % t, False),
                                                 ("fz", "rz", "zl%d" % t, "az%d" % t, False)):
                g.wait_ge(T.sem[sem], n_in)
                a, b = T[there][:], T[here][:]
                if codes:
                    a, b = a.bitcast(dt.uint8), b.bitcast(dt.uint8)
                g.remote_dma(a, b, T.sem[arr], T.sem.sent, pid, rid, mask)
            g.wait_ge(T.sem.sent, 3 * n_out)


def rank_program(g, core, T, topo):
    rank = T.rank_of(core)
    if rank is None:
        _hand_on(g, core, T, topo)
        return
    cores = list(T.cores)
    ops = []
    sent, outs = [0], [0]

    def ap(name, lo=0, hi=None, step=1):
        hi = SCRATCH[name][1][1] if hi is None else hi
        kind = 2 if SCRATCH[name][2] == BF else 4
        mask = 0
        if step == 1 or step == -1:
            mask = ((1 << (hi - lo)) - 1) << lo
        else:
            for c in range(lo, hi, step):
                mask |= 1 << c
        if step == -1:
            v = T[name][:, slice(hi - 1, lo - 1 if lo else None, -1)]
        elif step == 1:
            v = T[name][:, lo:hi]
        else:
            v = T[name][:, lo:hi:step]
        return (v, [(name, mask)], len(range(lo, hi, abs(step))), kind)

    def col(name, c):
        return ap(name, c, c + 1)

    def bank(b, lo, hi, step=1):
        v = T.ps[:, 512 * b + lo:512 * b + hi] if step == 1 else T.ps[:, 512 * b + lo:512 * b + hi:step]
        return (v, [("ps#%d" % b, 1)], len(range(lo, hi, step)), "p")

    def ind(win, off):
        return (win[0].indirect(off[0]), win[1] + off[1], 16 * off[2], "i")

    def add(eng, fn, writes, reads, cycles, late=0.0, **kw):
        acc = [(n, m, True) for o in writes for n, m in o[1][:1]] + [(n, m, False) for o in writes for n, m in o[1][1:]]
        acc += [(n, m, False) for o in reads if isinstance(o, tuple) for n, m in o[1]]
        ops.append(dict(eng=eng, fn=fn, acc=acc, busy=max(cycles, LEAST) * CYC + FIX, late=late, **kw))

    def raw(o):
        return o[0] if isinstance(o, tuple) else o

    def rate(out, *ins):
        if out[3] == "i":
            return 35 + 2.9 * out[2]
        if ins and ins[0][3] == "i":
            return 35 + 1.25 * out[2]
        return (0.5 if all(o[3] == 2 for o in (out,) + ins) else 1.0) * max([out[2]] + [o[2] for o in ins])

    def tt(out, a, b, op):
        add("V", lambda q: q.tensor_tensor(out[0], a[0], b[0], op), [out], [a, b], rate(out, a) if a[3] == "i" else out[2] * (1.0 if a[3] == "p" else 2.0))

    def ts(out, a, s1, op0, s2=None, op1=None):
        if op1 is None:
            add("V", lambda q: q.tensor_scalar(out[0], a[0], raw(s1), None, op0), [out], [a, s1], rate(out, a))
        else:
            add("V", lambda q: q.tensor_scalar(out[0], a[0], raw(s1), raw(s2), op0, op1), [out], [a, s1, s2], rate(out, a))

    def cp(out, a):
        add("V", lambda q: q.tensor_copy(out[0], a[0]), [out], [a], rate(out, a))

    def turn(out, a):
        add("V", lambda q: q.transpose(out[0], a[0]), [out], [a], rate(out, a))

    def scan(out, a, b, init, op0, op1):
        add("V", lambda q: q.tensor_tensor_scan(out[0], a[0], b[0], raw(init), op0, op1), [out], [a, b, init], rate(out, a, b))

    def red(out, a, op):
        add("V", lambda q: q.tensor_reduce(out[0], a[0], AxisListType.X, op), [out], [a], a[2])

    def fill(out, v):
        add("V", lambda q: q.memset(out[0], v), [out], [], rate(out))

    def quant(qn, sn, lo, hi, src):
        a, b = ap(qn, lo, hi), ap(sn, lo, hi)
        add("V", lambda q: q.quantize_mx(a[0], b[0], src[0]), [a, b], [src], 0.27 * src[2])

    def act(out, a, func, bias=0.0, scale=1.0, accum=None):
        c = 50 + 1.25 * out[2] if a[3] == "i" else out[2]
        if accum is None:
            add("S", lambda q: q.activation(out[0], a[0], func, bias=raw(bias), scale=raw(scale)), [out], [a, bias, scale], c)
        else:
            add("S", lambda q: q.activation(out[0], a[0], func, bias=raw(bias), scale=raw(scale), accum_out=accum[0]), [out, accum], [a, bias, scale], c + 25)

    def mm(b, sq, ss, s0, mq, ms, lo, hi, start=True, stop=True):
        out, a, sa, m, sm = bank(b, 0, hi - lo), ap(sq, s0, s0 + 128), ap(ss, s0, s0 + 128), ap(mq, lo, hi), ap(ms, lo, hi)
        add("P", lambda q: q.matmul_mx(out[0], a[0], sa[0], m[0], sm[0], start, stop), [out], [a, sa, m, sm], 0.6 * (hi - lo + 16), late=60.0, chain=not start)

    def iota(out, pattern, base, cm, small=True):
        if small:
            add("G", lambda q: q.iota(out[0], pattern, base, cm, allow_small_or_imprecise_dtypes=True), [out], [], 2 * out[2] + 120)
        else:
            add("G", lambda q: q.iota(out[0], pattern, base, cm), [out], [], 2 * out[2] + 120)

    def keep(out, a, pattern, op, base, cm):
        add("G", lambda q: q.affine_select(out[0], a[0], pattern, op, 0.0, base, cm), [out], [a], 2 * out[2] + 160)

    def load(eng, out, src, sem, codes=False, after=(), n=16):
        o = out[0].bitcast(dt.uint8) if codes else out[0]
        add(eng, lambda q: q.dma_start(o, src), [out], list(after), 60, late=DMA + out[2], sem=sem, n=n, inc=sem)

    def add_into(out, a, sem):
        add("G", lambda q: q.dma_start(out[0], a[0], accum_op=A.add), [out], [a], 300, late=DMA + 2.5 * out[2], sem=sem, n=16, inc=sem)

    def store(eng, dst, src, reads):
        outs[0] += 16
        add(eng, lambda q: q.dma_start(dst, src), [], [reads], 60, late=DMA + reads[2], inc="out", sem="out", n=0)

    def send(t, here, there, hop, arr, hopsem, codes=False):
        dst = cores[rank ^ (1 << t)]
        via = _relay(core, dst, cores, topo)
        to, name, sem = (dst, there, arr) if via is None else (via, hop, hopsem)
        rid, pid = topo.addr(to, core)
        mask = topo.mask(core, to)
        a, b = T[name][:], here[0]
        if codes:
            a, b = a.bitcast(dt.uint8), b.bitcast(dt.uint8)
        sent[0] += _width(topo, core, to)
        add("G", lambda q: q.remote_dma(a, b, T.sem[sem], T.sem.sent, pid, rid, mask), [], [here], 500, sem="sent", n=0)
        back = _relay(dst, core, cores, topo)
        add(None, None, [ap(there)], [], 0, late=(HOP + (3000.0 if codes else 0.0)) * (1 if back is None else 2), follow=len(ops) - 1,
            sem=arr, n=_width(topo, dst if back is None else back, core))

    def scores(t, tq, tp, h):
        lo, hi = HALVES[t][h]
        mm(h, "upq", "ups", 0, tq, tp, lo, hi)
        mm(5 + h, "upq", "ups", 0, tq, tp, lo, hi)

    def lengths(k, row, lo=0, hi=W):
        return ap("dd", D0 + SEG * k + W * row + lo, D0 + SEG * k + W * row + hi)

    cut = 4 * RUNS[0][1]
    load("Y", ap("xa", cut, 4 * C), T.x[:, cut:4 * C], "ldxa")
    load("S", ap("ub"), T.u[:, :], "ldu")
    load("S", ap("xa", 0, cut), T.x[:, 0:cut], "ldxb")
    iota(ap("ui"), [[16, 8]], 0, 0, small=False)
    iota(ap("i2"), [[-1, C]], 512, 1, small=False)
    fill(ap("ones"), 1.0)
    fill(ap("mt", 0, 8 * W), 0.0)
    keep(ap("ba"), ap("ones"), [[16, 8], [0, 64]], A.is_ge, 15, -1)
    keep(ap("bt"), ap("ba"), [[-16, 8], [0, 64]], A.is_ge, 0, 1)
    cp(ap("uoff"), ap("ui"))
    fill(ap("mt", 0, 8 * W, 65), -256.0)
    ts(ap("i2a"), ap("i2"), 15, A.bitwise_and)
    ts(ap("m16"), ap("i2a"), -2 * BIG, A.mult, BIG, A.add)
    act(ap("c1", 12 * H, 14 * H), ap("ones", 0, 2 * H), F.Copy, scale=0.0)
    act(ap("c1", 14 * H, 16 * H), ap("ones", 0, 2 * H), F.Copy, scale=0.0)
    act(ap("c2", 1024, 1536), ap("ones"), F.Copy, scale=0.0)
    quant("uq", "us", 0, 128, ap("ub"))
    o1, w1, o2, w2 = ap("upq"), ap("uq"), ap("ups"), ap("us")
    add("V", lambda q: q.tensor_copy(o1[0].bitcast(dt.uint32), w1[0].bitcast(dt.uint32).indirect(T.uoff[:, 0:8])), [o1], [w1, ap("uoff")], 200)
    add("S", lambda q: q.activation(o2[0], w2[0].indirect(T.uoff[:, 0:8]), F.Copy), [o2], [w2, ap("uoff")], 200)
    for h, (lo, hi) in enumerate(HALVES[0]):
        quant("tq0", "ts0", lo, hi, ap("xa", 4 * lo, 4 * hi))
        scores(0, "tq0", "ts0", h)
    fill(ap("zer"), 0.0)
    fill(ap("rst2"), 0.0)
    fill(ap("rst2", 0, H, 16), -BIG)
    wide = max(HALVES[t][h][1] - HALVES[t][h][0] for t in range(R) for h in DIRECT[t])
    for e in range(2):
        act(ap("m32", e, wide, 2), ap("m16", 0, wide // 2), F.Copy)
        act(ap("rst1", e, wide, 2), ap("rst2", 0, wide // 2), F.Copy, scale=1.0 - e)
    fill(lengths(0, 0), 128.0)
    for k in range(1, 4):
        load("Y", ap("mt", 8 * W * k, 8 * W * (k + 1)), T.mt[:, 0:8 * W], "mfill", after=[ap("mt", 0, 8 * W), ap("xa")], n=16 * 3)
    load("Y", ap("wq"), T.wc[:, :], "ldw", codes=True, after=[ap("xa")])
    load("Y", ap("vb"), T.v[:, :], "ldv", after=[ap("xa")])
    load("G", ap("wp"), T.ws[:, :], "ldp", after=[ap("xa")])
    iota(ap("nw"), [[-2, H]], 511, 0)
    iota(ap("rt", K, 2 * K), [[W, S], [K, 2]], 0, 0)
    quant("bq", "bs", 0, 128, ap("bt"))
    for c in range(4):
        ts(col("thr", c), col("i2a", 0), -1.0, A.mult, -0.5 - 16 * c, A.add)
        keep(ap("et", 512 * c, 512 * c + 512), ap("ones"), [[1, 512]], A.is_equal, -c, -4)
    act(ap("rt", 0, K), ap("rt", K, 2 * K), F.Identity, bias=-512.0, scale=1024.0)
    ts(col("par", 0), col("i2a", 0), 1, A.bitwise_and)
    ts(col("pc", 0), col("par", 0), -float(K), A.mult, 1.0, A.add)
    ts(col("pc", 1), col("par", 0), float(K), A.mult, S * W - 0.5, A.add)
    if SPLIT:
        for k in range(2):
            fill(lengths(k, HS + 1, 0, SEG - (HS + 1) * W), 0.0)
            iota(ap("edge", W * (k + 2), W * (k + 2) + 65), [[1, 65]], 8 * W * (k + 2), 0)
            iota(ap("edge", W * (k + 2) + 65, W * (k + 3)), [[-1, 65]], 8 * W * k + K - 1, 0)
        ts(col("pc", 2), col("i2a", 0), 65.0, A.mult, col("pc", 0), A.add)
        ts(col("pc", 2), col("pc", 2), 1024.0, A.mult, -1024.0, A.add)
        ts(col("pc", 3), col("par", 0), 1024.0 * (K - 1), A.mult, col("pc", 2), A.add)
        ts(col("pc", 2), col("pc", 3), 512.0, A.add)
        for k in range(2):
            act(ap("edge", W * k, W * k + 65), ap("edge", W * (k + 2), W * (k + 2) + 65), F.Identity, bias=col("pc", 2), scale=1024.0)
            act(ap("edge", W * k + 65, W * k + W), ap("edge", W * (k + 2) + 65, W * (k + 3)), F.Identity, bias=col("pc", 3), scale=1024.0)
        ts(col("pc", 4), col("i2a", 0), 15.0, A.is_equal)
        for c, v in ((5, UP), (6, -128.25), (7, -128.5)):
            act(col("pc", c), col("pc", 4), F.Copy, scale=v)
        fill(ap("rst3"), 0.0)
        fill(ap("rst3", 0, 128, 32), -BIG)
        fill(ap("lt", 1, 128, 2), 0.0)
        fill(ap("lt", 31, 128, 32), -BIG)
    act(ap("m16b"), ap("m16"), F.Copy)
    for wn in ("wn0", "wn1"):
        act(ap(wn, 0, WN), ap("ones", 0, WN), F.Copy, scale=0.0)
        act(ap(wn, WN, 2 * WN), ap("ones", 0, WN), F.Copy)

    def planes(row, n, hold, step, tile, qn, sn, b, aside):
        nc = n // 16
        tiles = nc // 4 + 1

        def pivot(c):
            return col(hold, step * 16 * (c + 1) - 1)

        def part(c, lo, hi):
            at = 4 * n * (c // 4) + c % 4
            return ap(tile, at + 4 * lo, at + 4 * hi - 3, 4)

        for k, c in enumerate(aside):
            e = 16 * (c + 1)
            act(ap("sg", n * k, n * k + n), ap(row), F.Sign, bias=pivot(c), scale=-1.0)
            act(part(c, 0, e), ap("sg", n * k, n * k + e), F.Relu)
            if e < n:
                act(part(c, e, n), ap("sg", n * k + e, n * k + n), F.Sign, bias=1.0)
        tt(part(nc, 0, n), ap(row), ap(hold, step - 1, step * n, step), A.is_equal)
        order = sorted(range(tiles), key=lambda m: (len([c for c in aside if c // 4 == m]), -m))
        for m in order:
            for c in range(4 * m, min(4 * m + 4, nc)):
                if c in aside:
                    continue
                e = 16 * (c + 1)
                ts(part(c, 0, e), ap(row, 0, e), pivot(c), A.is_lt)
                if e < n:
                    ts(part(c, e, n), ap(row, e, n), pivot(c), A.is_le)
            quant(qn, sn, n * m, n * m + n, ap(tile, 4 * n * m, 4 * n * m + 4 * n))
            mm(b, "bq", "bs", 0, qn, sn, n * m, n * m + n, m == order[0], m == order[-1])

    def chosen(row, n, unit, off, on_scalar):
        w = n - K + 16
        for c in range(4):
            junk = ap("junk", H * c, H * c + w)
            if c < on_scalar:
                act(junk, ap(row, 16 * c, 16 * c + w), F.Sign, bias=col("thr", c), scale=unit, accum=col("acc", c))
                ts(col(off, c), col("acc", c), -0.5, A.mult, 16 * c + w / 2, A.add)
            else:
                ts(junk, ap(row, 16 * c, 16 * c + w), col("thr", c), A.add, 0.0, A.is_lt)
                scan(ap("junk2", H * (c % 2), H * (c % 2) + w), junk, ap("zer", 0, w), 16.0 * c, A.add, A.add)
                cp(col(off, c), col("junk2", H * (c % 2) + w - 1))

    def split_chain():
        for k in range(2):
            ts(lengths(k + 1, 0, 0, 65), ap("edge", W * k, W * k + 65), col("th", 16 * (k + 2) + 15), A.is_gt, 128.0, A.mult)
            ts(lengths(k + 1, 0, 65, W), ap("edge", W * k + 65, W * k + W), col("th", 16 * k + 15), A.is_lt, 128.0, A.mult)
            act(ap("neg", W * k, W * k + W), lengths(k + 1, 0), F.Copy, scale=-2.0)
        for j in range(HS):
            for k in range(3):
                first = j + (HS if k else 0)
                scan(lengths(k, j + 1), ap("mt", W * first, W * first + W), lengths(k, j), 0.0, A.add, A.max)
        at = D0 + W * HS
        for k in range(2):
            scan(ap("base", W * k, W * k + W, -1), ap("neg", W * k, W * k + W, -1), ap("dd", at, at + W, -1), 0.0, A.add, A.max)
        tt(ap("mid", 0, 65), ap("dd", at, at + 65), ap("dd", at + 65, at + W, -1), A.add)
        red(col("mid", 65), ap("mid", 0, 65), A.max)
        act(col("pm", 0), col("mid", 65), F.Identity, bias=1.0)
        ends = ap("dd", D0 + W, D0 + (HS + 1) * W)
        act(ap("ll", 0, S), ind(ends, ap("poff", 0, 2)), F.Identity, bias=col("pc", 6), scale=col("pc", 5))
        act(ap("ll", S, K), ind(ends, ap("poff", 6, 8)), F.Identity, bias=col("pc", 7), scale=col("pc", 4))
        turn(ap("lt", 0, 128, 2), ap("ll"))
        for k in range(2):
            at = D0 + SEG * (k + 1) + W - HS * W
            tab = ap("dd", at, at + S * W)
            act(ap("xs", K * k, K * k + S), ind(tab, ap("poff", 4, 6)), F.Identity, bias=col("base", W * k + 65))
            ts(ap("xs", K * k + S, K * k + K), ind(tab, ap("poff", 2, 4)), col("base", W * k), A.add, UP, A.mult)
            turn(ap("xt", k, 128, 2), ap("xs", K * k, K * k + K))
        scan(ap("xu"), ap("rst3"), ap("xt"), 0.0, A.add, A.max)
        scan(ap("xv", 0, 128, -1), ap("lt", 0, 128, -1), ap("xu", 0, 128, -1), 0.0, A.add, A.max)
        turn(ap("ss"), ap("xv", 0, 128, 2))

    state = "xa"
    for t in range(R):
        tq, tp, lq, lp, wn = "tq%d" % t, "ts%d" % t, "lq%d" % t, "ls%d" % t, "wn%d" % t
        send(t, ap(tq), lq, "rq", "aq%d" % t, "fq", codes=True)
        send(t, ap(tp), lp, "rs", "as%d" % t, "fs")
        for h, (lo, hi) in enumerate(HALVES[t]):
            a, b = lo // 2, hi // 2
            act(ap("po", a, b), bank(5 + h, 1, hi - lo, 2), F.Copy)
            tt(ap("wv", a, b), bank(h, 0, hi - lo, 2), ap("po", a, b), A.max)
            if h in DIRECT[t]:
                tt(ap("mk", lo, hi), bank(h, 0, hi - lo), ap("m32", 0, hi - lo), A.min)
                scan(ap("hold", lo, hi), ap("rst1", 0, hi - lo), ap("mk", lo, hi), 0.0, A.add, A.max)
            else:
                tt(ap("mk", lo, lo + b - a), ap("wv", a, b), ap("m16", a, b), A.min)
                scan(ap("hold", lo + 1, hi, 2), ap("rst2", a, b), ap("mk", lo, lo + b - a), 0.0, A.add, A.max)
            act(ap("pe", a, b), bank(5 + h, 0, hi - lo, 2), F.Copy)
        planes("wv", H, "hold", 2, "c1", "c1q", "c1s", 4, SCALAR_PIVOTS[0])
        ts(ap("sel"), bank(4, 0, H), K + 0.5, A.is_le)
        scan(ap("cnt"), ap("sel"), ap("zer"), 0.0, A.add, A.add)
        chosen("cnt", H, 1.0, "moff", COUNTS)
        for e, win in enumerate(("pe", "po")):
            tt(ap("mk2", e, 128, 2), ind(ap(win), ap("moff")), ap("m16", e, 128, 2), A.min)
            act(ap("cand", e, 128, 2), ind(ap(win), ap("moff")), F.Copy)
        act(ap("xc", 0, 128, 2), ind(ap("nw"), ap("moff")), F.Copy)
        act(ap("xc", 1, 128, 2), ind(ap("nw"), ap("moff")), F.Identity, bias=-1.0)
        tt(ap("dx", 1, 128), ap("xc", 1, 128), ap("xc", 0, 127), A.subtract)
        cp(col("dx", 0), col("xc", 0))
        scan(ap("hold2"), ap("rst2", 0, 128), ap("mk2"), 0.0, A.add, A.max)
        planes("cand", 128, "hold2", 1, "c2", "c2q", "c2s", 5, SCALAR_PIVOTS[1])
        tt(ap("mk3"), bank(5, 0, 128), ap("m16", 0, 128), A.min)
        ts(ap("sel", 0, 128), bank(5, 0, 128), K + 0.5, A.is_le, 1024.0, A.mult)
        scan(ap("hold3"), ap("rst2", 0, 128), ap("mk3"), 0.0, A.add, A.max)
        scan(ap("zr"), ap("sel", 0, 128), ap("dx"), -512.0, A.add, A.add)
        ts(ap("roff"), ap("hold3", 15, 128, 16), -1.0, A.add)
        act(ap("r2"), bank(5, 0, 128), F.Copy)
        cp(ind(ap("zs%d" % t), ap("roff")), ap("zr"))
        listed = len(ops) - 1
        send(t, ap("zs%d" % t, 0, K), "zl%d" % t, "rz", "az%d" % t, "fz")
        chosen("zr", 128, 1.0 / 1024, "yoff", 4)
        counted = len(ops) - 1
        tt(ap("km"), ind(ap("r2"), ap("yoff")), ap("m16", 0, K), A.min)
        tt(ap("am"), ind(ap("xc"), ap("yoff")), ap("m16", 0, K), A.min)
        scan(ap("kh"), ap("rst2", 0, K), ap("km"), 0.0, A.add, A.max)
        scan(ap("ah"), ap("rst2", 0, K), ap("am"), 0.0, A.add, A.max)
        ts(ap("koff"), ap("kh", 15, K, 16), -1.0, A.add)
        if t:
            cp(ind(ap("mt"), ap("poff")), ap("zer", 0, 128))
            ops[-1]["follow"] = listed
            quant("vq", "vs", 0, 128, ap("vb"))
        else:
            quant("eq", "es", 0, 512, ap("et"))
        ops[-1]["follow"] = listed
        act(ap("na"), ind(ap("xc"), ap("yoff")), F.Identity, bias=H + 1.0, scale=-1.0)
        ts(ap("aoff", 0, 4), ap("ah", 15, K, 16), -1.0, A.mult, 511.0, A.add)
        ts(ap("aoff", 4, 8), ap("ah", 15, K, 16), -1.0, A.mult, 511.0 + WN, A.add)
        zl = "zl%d" % t
        tt(ap("tz"), ind(ap(zl), ap("koff")), ap("rt", 0, K), A.add)
        scan(ap("th"), ap("m16", 0, K), ap("tz"), 0.0, A.max, A.min)
        tt(ap("dif"), ap("tz", 1, K, 2), ap("tz", 0, K, 2), A.subtract)
        ts(ap("poff", 0, 4), ap("th", 15, K, 16), 1.0 / 1024, A.mult, col("pc", 0), A.add)
        ts(ap("poff", 4, 8), ap("th", 15, K, 16), -1.0 / 1024, A.mult, col("pc", 1), A.add)
        for e in (0, 1, K, K + 1):
            ts(ap("bump", e, e // K * K + K, 2), ap("dif"), 1024.0 * K, A.is_gt, 0.625, A.max)
        cp(ind(ap("mt"), ap("poff")), ap("bump"))
        ts(ap("nb"), ind(ap(zl), ap("koff")), 511, A.bitwise_and)
        tt(ap("km"), ap("nb"), ap("na"), A.add)
        ts(ap("bc"), ap("nb"), -1.0 / 512, A.mult, (511.0 - H) / 512, A.add)
        for b in range(4):
            mm(4 + b, "eq", "es", 128 * b, lq, lp, 0, C)
            ops[-1]["follow"] = listed
            act(ap("xh", C * b, C * b + C), ap(state, C * b, C * b + C), F.Copy, scale=0.5)
            ops[-1]["follow"] = counted
            act(ap("dh", C * b, C * b + C), bank(4 + b, 0, C), F.Copy, scale=0.5)
            ops[-1]["follow"] = counted
        split_chain()
        scan(ap("pm", 1, K + 1), ap("ss"), ap("ss"), col("pm", 0), A.max, A.max)
        tt(ap("keep"), ap("pm", 0, K), ap("pm", 1, K + 1), A.is_equal)
        tt(ap("val", 0, K), ap("pm", 0, K), ap("pm", 1, K + 1), A.subtract)
        tt(ap("val", K, 2 * K), ap("keep"), ap("bc"), A.add)
        tt(ap("ll"), ap("val", 0, K), ap("km"), A.mult)
        cp(ind(ap(wn), ap("aoff")), ap("val"))
        scan(ap("xw", 0, K, -1), ap("keep", 0, K, -1), ap("ll", 0, K, -1), 0.0, A.mult, A.add)
        scan(ap("cap", 0, C, -1), ap(wn, 1, C + 1, -1), ap(wn, WN, WN + C, -1), (C - 1 - H) / 512.0, A.add, A.min)
        for lo, hi, qq, first in ((0, 128, "xu", col("xw", 0)), (128, C, "qq", col("xu", 127))):
            act(ap("gf", lo, hi), ap(wn, lo, hi), F.Identity, bias=1.0 / 512, scale=-8192.0)
            scan(ap(qq, lo, hi), ap("gf", lo, hi), ap("cap", lo, hi), first, A.add, A.min)
            scan(ap("qh", lo, hi), ap("m16b", lo, hi), ap(qq, lo, hi), -100.0, A.max, A.min)
            ts(ap("qoff", lo // 16, hi // 16), ap("qh", lo + 15, hi, 16), 512.0, A.mult, float(H), A.add)
            act(ap("qo", C * t + lo, C * t + hi), ap(qq, lo, hi), F.Relu, bias=float(H), scale=512.0)
        store("Y", T.oq[:, C * t:C * t + C], T.qo[0:128:16, C * t:C * t + C], ap("qo", C * t, C * t + C))
        packed = 0
        for h, (lo, hi) in enumerate(RUNS):
            for b in range(4):
                tt(ap("gt", 4 * lo + b, 4 * hi, 4), ind(ap("dh", C * b, C * b + C), ap("qoff", lo // 16, hi // 16)), ap("xh", 4 * lo + b, 4 * hi, 4), A.add)
                if h and b == 1:
                    ops[-1]["follow"] = packed
            packed = len(ops)
            quant("gq", "gs", lo, hi, ap("gt", 4 * lo, 4 * hi))
            for b in range(4):
                mm(4 * (h % 2) + b, "wq", "wp", 128 * b, "gq", "gs", lo, hi)
                act(ap("rl", 4 * lo + b, 4 * hi, 4), bank(4 * (h % 2) + b, 0, hi - lo), F.Relu, scale=0.015625)
            if lo < BY_DMA:
                add_into(ap("gt", 4 * lo, 4 * min(hi, BY_DMA)), ap("rl", 4 * lo, 4 * min(hi, BY_DMA)), "add%d%d" % (t, h))
            if hi > BY_DMA:
                for b in range(4):
                    part = ap("gt", 4 * max(lo, BY_DMA) + b, 4 * hi, 4)
                    tt(part, ap("rl", 4 * max(lo, BY_DMA) + b, 4 * hi, 4), part, A.add)
        state, tq, tp = "gt", "tq%d" % (t + 1), "ts%d" % (t + 1)
        for h, (lo, hi) in enumerate(RUNS):
            quant(tq, tp, lo, hi, ap(state, 4 * lo, 4 * hi))
            if t == R - 1:
                mm(h, "vq", "vs", 0, tq, tp, lo, hi)
                store("Y", T.oc[:, 4 * lo:4 * hi], T[tq][:, lo:hi].bitcast(dt.uint8), ap(tq, lo, hi))
                act(ap("yb", lo, hi), bank(h, 0, hi - lo), F.Copy)
                store("S", T.y[:, lo:hi], T.yb[:, lo:hi], ap("yb", lo, hi))
            else:
                scores(t + 1, tq, tp, h)
    for k in range(4):
        store("Y", T.osc[4 * k:4 * k + 4, :], T.ts2[32 * k:32 * k + 4, :], ap("ts2"))
    _emit(g, T, _arrange(ops), [("G", "sent", sent[0]), ("Y", "out", outs[0])])
